import numpy as np, ml_dtypes
CORES = [35,38,43,46]
N = 4
BF = ml_dtypes.bfloat16
def gentries(a):
    return np.ascontiguousarray(a.reshape(8, 16, -1).transpose(0, 2, 1)).reshape(8, -1)
def gtable(e):
    e = np.asarray(e); return np.ascontiguousarray(e.reshape(8, -1, 16).transpose(0, 2, 1)).reshape(128, -1).astype(np.int32)
P, C, CAP, TH, DAYS, BITS = 1024, 4, 384, 1200, 4, 11
W = N * P; M = 2 ** BITS; B0 = TH // 16; DEC = 8; STEP = 77
def parts(rng):
    x = (rng.random((N, 8, 16, P)) * B0 * rng.random((N, 8, 1, P))).astype(np.int64); x = np.minimum(x, B0 - 1)
    return x, rng.integers(0, W, (N, 8, C * P)), rng.integers(0, M, (N, 8, C * P)), rng.integers(0, 256, (N, 8, P))
def even(rng):
    u = rng.integers(-B0, B0 + 1, (N, 8, 8, P)); u[:, :, 0] = np.abs(u[:, :, 0])
    return np.concatenate([B0 + u, B0 - u], axis=2)
def sick(rng):
    e = even(rng)
    return np.minimum(e + ((256 - e) * rng.random((N, 8, 1, P)) * rng.random(e.shape)).astype(np.int64), 255)
def lean(rng):
    n = rng.integers(-(-TH // 255), 9, (N, 8, 1, P)); s = rng.integers(0, 16, (N, 8, 1, P)); lo = -(-TH // n)
    on = (np.arange(16)[:, None] - s) % 16 < n
    return np.where(on, np.minimum(lo + ((256 - lo) * rng.random((N, 8, 16, P))).astype(np.int64), 255), 0)
def mark(rng, x, share):
    return np.where(rng.random((N, 8, 1, P)) < share, sick(rng), x)
def pack(x, nb, dice, res):
    return {"x0": np.ascontiguousarray(x.reshape(N, 128, P)).astype(np.int32), "nb": np.stack([gtable(v) for v in nb]), "dice": np.stack([gtable(v) for v in dice]), "res": np.ascontiguousarray(res).astype(np.int32)}
def setup_inputs(rng):
    x, nb, dice, res = parts(rng); share = rng.choice(np.array([0.04, 0.1, 0.2, 0.45]), (N, 8, 1, 1))
    return pack(mark(rng, x, share), nb, dice, res)
def setup_inputs_room(rng):
    x, nb, dice, res = parts(rng); m = np.zeros((N, 8, P), bool)
    n = rng.choice(np.array([0, 1, CAP - 1, CAP, CAP + 1, P]), (N, 8))
    n[0] = (CAP, CAP + 1, P, CAP - 1, 1, 0, CAP, CAP + 1)
    n[1] = (0, P, CAP + 1, 1, CAP - 1, CAP, CAP, CAP)
    n[2] = (CAP, CAP + 1, CAP, P, CAP, CAP + 1, CAP, CAP)
    n[3, ::2] = CAP
    j = P - CAP; cnt = W - int(np.sum(np.minimum(n[:, 6], CAP)))
    while -(-j * M // cnt) * cnt >= (j + 1) * M: j += 1; cnt += 1
    n[0, 6] = P - j; d = -(-j * M // cnt)
    for q in range(N):
        for g in range(8):
            o = rng.permutation(P)
            if (q == 0 and g >= 6) or (q == 1 and g == 7): o = np.arange(P)[::-1]
            if (q == 1 and g == 6) or (q == 2 and g == 7): o = np.arange(P)
            if q == 3: o = np.argsort(rng.permutation(16)[np.arange(P) % 16], kind="stable")
            m[q, g, o[:int(n[q, g])]] = True
    x = np.where(m[:, :, None, :], sick(rng), x)
    x[:, 6] = np.where(m[:, 6][:, None, :], even(rng)[:, 6], x[:, 6]); res[:, 6] = 255
    dice[:, 6] = np.where(rng.random((N, C * P)) < 0.1, d, dice[:, 6])
    return pack(x, nb, dice, res)
def setup_inputs_ties(rng):
    x, nb, dice, res = parts(rng)
    x = np.where(rng.random((N, 8, 1, P)) < 0.2, rng.choice(np.array([0, 7, 8, 9]), x.shape), x)
    x = mark(rng, x, 0.06); e = even(rng); e[:, :, 0] += rng.integers(-1, 2, (N, 8, P))
    x = np.where(rng.random((N, 8, 1, P)) < 0.35, e, x)
    x = np.where(rng.random((N, 8, 1, P)) < 0.08, lean(rng), x)
    res = np.where(rng.random(res.shape) < 0.7, rng.choice(np.array([0, 1, 7, 8, 9, 255]), res.shape), res)
    return pack(x, nb, dice, res)
def setup_inputs_ends(rng):
    x, nb, dice, res = parts(rng); x = mark(rng, x, 0.15); s = sick(rng)
    x[..., 0] = s[..., 0]; x[..., P - 1] = s[..., P - 1]
    nb[:, 1::2] = np.tile(nb[:, 1::2, :P], (1, 1, C))
    nb[:, 2] = rng.choice(np.array([0, P - 1, W - P, W - 1]), (N, C * P))
    nb[:, 4] = P * np.arange(N)[:, None] + rng.integers(0, P, (N, C * P))
    me = P * np.arange(N)[:, None] + np.tile(np.arange(P), C)[None, :]
    nb[:, 6] = np.where(rng.random((N, C * P)) < 0.5, me, nb[:, 6])
    dice = np.where(rng.random(dice.shape) < 0.8, rng.choice(np.array([0, 1, M - 1, M - 2, M - STEP, M - STEP - 1, M - 2 * STEP, M // 2]), dice.shape), dice)
    return pack(x, nb, dice, res)
def setup_inputs_cold(rng):
    x, nb, dice, res = parts(rng); share = rng.choice(np.array([0.05, 0.15, 0.3]), (N, 8, 1, 1))
    q = rng.permutation(N); c = rng.permutation(8)
    share[q[0]] = 1.0; share[q[1]] = 0.0; share[:, c[0]] = 0.0; share[:, c[1]] = 1.0; share[:, c[[2, 4, 5]]] = 0.0
    x = mark(rng, x, share); e = even(rng)
    a, v = int(rng.integers(0, N)), int(rng.integers(0, P)); x[a, c[2], :, v] = 255
    late = rng.random((N, 1, P)) < 0.25; last = np.arange(C)[:, None] == C - 1
    nb[:, c[2]] = np.where((last | ~late).reshape(N, C * P), a * P + v, nb[:, c[2]])
    nb[q[1], c[3]] = q[0] * P + rng.integers(0, CAP, C * P)
    h = rng.random((N, 1, P)) < 0.2; stay = rng.random((N, 1, P)) < 0.5; stay[q[2]] = False
    x[:, c[4]] = np.where(h, np.where(stay, 255, e[:, c[4]]), x[:, c[4]]); res[:, c[4]] = 255
    h = rng.random((N, P)) < 0.1; u = np.arange(W).reshape(N, P)
    x[:, c[5]] = np.where(h[:, None, :], rng.integers(min(B0 + DEC * DAYS, 255), 256, (N, 16, P)), x[:, c[5]]); res[:, c[5]] = rng.integers(0, 32, (N, P))
    nb[:, c[5]] = np.where(np.tile(h, (1, C)), rng.choice(u[h], (N, C * P)), rng.choice(u[~h], (N, C * P)))
    return pack(x, nb, dice, res)
def setup_inputs_spread(rng):
    x, nb, dice, res = parts(rng)
    x = np.minimum((np.exp2(8 * rng.random((N, 8, 1, P))) * rng.random((N, 8, 16, P))).astype(np.int64), 255)
    res = np.minimum(np.exp2(8 * rng.random((N, 8, P))).astype(np.int64) - 1, 255)
    nb = np.minimum((W * rng.random((N, 8, C * P)) ** rng.choice(np.array([1, 2, 3]), (N, 8, 1))).astype(np.int64), W - 1)
    dice = np.minimum((M * rng.random((N, 8, C * P)) ** 2).astype(np.int64), M - 1)
    return pack(x, nb, dice, res)
def check_inputs(d):
    bad = []
    for k, hi in (("x0", 255), ("nb", W - 1), ("dice", M - 1), ("res", 255)):
        if np.min(d[k]) < 0 or np.max(d[k]) > hi: bad.append("range of " + k)
    return bad
def reference(x0, nb, dice, res):
    x = x0.astype(np.int64).reshape(N, 8, 16, P); r = res.astype(np.int64).reshape(N, 8, 1, P)
    link = np.stack([gentries(v) for v in nb]).astype(np.int64); dr = np.stack([gentries(v) for v in dice]).astype(np.int64)
    for t in range(DAYS):
        high = (np.add.reduce(x, axis=2) >= TH).astype(np.int64); before = np.add.accumulate(high, axis=2) - high
        ill = (high == 1) & (before < CAP)
        flag = np.ascontiguousarray(ill.transpose(1, 0, 2)).reshape(8, W)
        win = np.ascontiguousarray(np.where(ill[:, :, None, :], x, 0).transpose(1, 2, 0, 3)).reshape(8, 16, W)
        come = []
        for q in range(N):
            come.append(np.maximum.reduce(np.take_along_axis(win, link[q][:, None, :], 2).reshape(8, 16, C, P), axis=2))
        d = (dr + STEP * t) & (M - 1); new = link.copy()
        for g in range(8):
            sl = np.flatnonzero(~flag[g])
            hit = flag[g][link[:, g]] & ~np.tile(ill[:, g], (1, C))
            new[:, g] = np.where(hit, sl[(d[:, g] * len(sl)) >> BITS], link[:, g])
        x = np.maximum(np.maximum(x - DEC, np.stack(come) - r), 0); link = new
    return {"yx": x.reshape(N, 128, P).astype(np.float32), "ynb": np.stack([gtable(v) for v in link]).astype(np.float32)}

@@ -1,0 +1,422 @@
+from concourse.bass import DstId, RemoteDMATransfer
+from concourse.mybir import AluOpType as A, AxisListType, ActivationFunctionType as F
+
+DAYS, P, CAP, TH, STEP, M2 = 4, 1024, 384, 1200, 77, 2047
+H = 512
+EPS = 2.0 ** -12
+SH = 8192.0
+SCRATCH = {
+    "xi": ("sbuf", [128, P], "int32"), "ni": ("sbuf", [128, 256], "int32"), "di": ("sbuf", [128, 256], "int32"),
+    "dtmp": ("sbuf", [128, 256], "int32"), "ri": ("sbuf", [8, P], "int32"), "rneg": ("sbuf", [8, P], "bfloat16"),
+    "xa": ("sbuf", [128, P], "bfloat16"), "xc": ("sbuf", [128, P], "bfloat16"), "xm": ("sbuf", [128, P], "bfloat16"),
+    "mm": ("sbuf", [128, P], "bfloat16"), "raw": ("sbuf", [128, 4 * P], "bfloat16"), "rsl": ("sbuf", [128, 4 * P], "bfloat16"),
+    "yo": ("sbuf", [128, P], "float32"), "no": ("sbuf", [128, 256], "float32"),
+    "off": ("sbuf", [128, 256], "uint16"), "offs": ("sbuf", [128, 256], "uint16"), "pos16": ("sbuf", [128, 64], "uint16"),
+    "ll": ("sbuf", [128, 256], "float32"), "lk": ("sbuf", [128, 256], "float32"), "h2": ("sbuf", [128, 256], "bfloat16"),
+    "yy": ("sbuf", [128, 256], "float32"), "hh": ("sbuf", [128, 256], "float32"), "oi": ("sbuf", [128, 256], "int32"),
+    "high": ("sbuf", [128, 64], "bfloat16"), "ill": ("sbuf", [128, 64], "bfloat16"), "pre": ("sbuf", [128, 64], "float32"),
+    "zz": ("sbuf", [128, 64], "float32"), "cum": ("sbuf", [128, 64], "float32"), "ee": ("sbuf", [128, 64], "float32"),
+    "pos": ("sbuf", [128, 64], "float32"), "z64": ("sbuf", [128, 64], "float32"), "vvc": ("sbuf", [128, 64], "float32"),
+    "vv": ("sbuf", [128, 64], "float32"), "cw": ("sbuf", [128, 4], "float32"), "cnt": ("sbuf", [128, 16], "float32"),
+    "col": ("sbuf", [128, 16], "float32"), "pmi": ("sbuf", [128, 1], "int32"), "pmf": ("sbuf", [128, 4], "float32"),
+    "t1": ("sbuf", [128, 128], "int32"), "t2": ("sbuf", [128, 128], "int32"), "t2s": ("sbuf", [128, 128], "int32"),
+    "t3": ("sbuf", [128, 16], "int32"), "r16": ("sbuf", [128, 16], "float32"), "t5": ("sbuf", [8, 128], "int32"),
+    "er": ("sbuf", [8, 128], "bfloat16"), "mb": ("sbuf", [128, 128], "bfloat16"), "idn": ("sbuf", [128, 128], "bfloat16"),
+    "ineg": ("sbuf", [128, 128], "bfloat16"), "ihalf": ("sbuf", [128, 128], "bfloat16"), "su": ("sbuf", [128, 128], "bfloat16"),
+    "su1": ("sbuf", [128, 128], "bfloat16"), "i2": ("sbuf", [128, 128], "bfloat16"), "su2": ("sbuf", [128, 128], "bfloat16"),
+    "bp": ("sbuf", [128, 144], "bfloat16"), "cp": ("sbuf", [128, 144], "bfloat16"), "ex": ("sbuf", [128, 2048], "bfloat16"),
+    "dat": ("sbuf", [128, P], "bfloat16"), "lo": ("sbuf", [8, P], "bfloat16"),
+}
+for _t in range(DAYS):
+    SCRATCH["win%d" % _t] = ("sbuf", [128, 4 * P], "bfloat16")
+    SCRATCH["sw%d" % _t] = ("sbuf", [128, 4 * P], "bfloat16")
+for _t in range(1, DAYS):
+    SCRATCH["dd%d" % _t] = ("sbuf", [128, 256], "int32")
+for _b in ("c0", "c1", "c2", "e0", "e1", "ht", "sl", "tc"):
+    SCRATCH[_b] = ("psum", [128, 512], "float32")
+SEMAPHORES = ["pv", "ps", "pp", "pg", "sent"] + ["dm%d" % i for i in range(12)]
+SEMAPHORES += [k + "%d" % t for k in ("al", "ac", "as") for t in range(DAYS)]
+
+
+def plan(topo, cores, src):
+    far = [d for d in cores if d != src and topo.chip(d) != topo.chip(src)]
+    near = [d for d in cores if d != src and topo.chip(d) == topo.chip(src)]
+    e = {}
+    used = []
+    for n, d in enumerate(far):
+        es = topo.engines(src, d)
+        w = len(es) // len(far)
+        e[d] = es[n * w:(n + 1) * w]
+        used += e[d]
+    for n, d in enumerate(near):
+        es = [x for x in topo.engines(src, d) if x not in used]
+        w = len(es) // len(near)
+        e[d] = es[n * w:(n + 1) * w]
+    return e
+
+
+def rank_program(g, core, T, topo):
+    q = T.rank_of(core)
+    if q is None:
+        return
+    cores = list(T.cores)
+    eng = {c: plan(topo, cores, c) for c in cores}
+    queue = {"V": g.vector, "S": g.scalar, "P": g.tensor, "G": g, "Y": g.sync}
+    psem = {"V": "pv", "S": "ps", "P": "pp", "G": "pg"}
+    done = {k: 0 for k in queue}
+    known = {k: {} for k in queue}
+    lastw, readers = {}, {}
+    ndma = [0]
+    nsent = [0]
+
+    def sync_to(qn, toks):
+        need = {}
+        for t in toks:
+            if known[qn].get(t[0], 0) < t[1]:
+                if t[1] > need.get(t[0], (0,))[0]:
+                    need[t[0]] = (t[1], t)
+        for s in sorted(need):
+            v, t = need[s]
+            if any(o != s and need[o][1][2].get(s, 0) >= v for o in need):
+                continue
+            queue[qn].wait_ge(T.sem[s], v)
+        for s in need:
+            v, t = need[s]
+            for k2, v2 in t[2].items():
+                if known[qn].get(k2, 0) < v2:
+                    known[qn][k2] = v2
+            if known[qn].get(s, 0) < v:
+                known[qn][s] = v
+
+    def deps(qn, reads, writes, accum):
+        toks = [lastw[k] for k in reads if k in lastw]
+        for k in writes:
+            if k in lastw and not (accum and lastw[k][3] == qn):
+                toks.append(lastw[k])
+            toks += [t for t in readers.get(k, []) if t[3] != qn]
+        sync_to(qn, toks)
+
+    def record(tok, reads, writes):
+        for k in reads:
+            readers.setdefault(k, []).append(tok)
+        for k in writes:
+            lastw[k] = tok
+            readers[k] = []
+
+    def emit(qn, fn, reads, writes, accum=False):
+        deps(qn, reads, writes, accum)
+        s = psem[qn]
+        fn().then_inc(T.sem[s], 1)
+        done[qn] += 1
+        record((s, done[qn], dict(known[qn]), qn), reads, writes)
+
+    def dma(qn, out, in_, reads, writes):
+        deps(qn, reads, writes, False)
+        s = "dm%d" % ndma[0]
+        ndma[0] += 1
+        queue[qn].dma_start(out, in_).then_inc(T.sem[s], 16)
+        tok = (s, 16, dict(known[qn]), None)
+        record(tok, reads, writes)
+        return tok
+
+    def send(dst_ap, src_ap, sem, reads):
+        deps("G", reads, [], False)
+        tr = []
+        for d in cores:
+            if d == core:
+                continue
+            rid, pid, se = topo.addr(d)
+            es = eng[core][d]
+            tr.append(RemoteDMATransfer(src=src_ap, dst=dst_ap, dst_ids=[DstId(rid=rid, pnc=pid)],
+                                        dma_engine_mask=sum(1 << x for x in es), remote_sem=T.sem[sem]))
+            nsent[0] += len(es)
+        g.remote_dma_fused(tr, local_sem=T.sem.sent)
+
+    arrive = sum(len(eng[c][core]) for c in cores if c != core)
+    for t in range(DAYS):
+        lastw[("win", t, "rem")] = ("al%d" % t, arrive, {}, None)
+        lastw[("cnt", t)] = ("ac%d" % t, arrive, {}, None)
+        lastw[("sw", t, "rem")] = ("as%d" % t, arrive, {}, None)
+
+    def ts(out, in0, s1, op0, r, w, s2=None, op1=None):
+        if op1 is None:
+            emit("V", lambda: g.vector.tensor_scalar(out, in0, s1, None, op0), r, w)
+        else:
+            emit("V", lambda: g.vector.tensor_scalar(out, in0, s1, s2, op0, op1), r, w)
+
+    def tt(out, a, b, op, r, w):
+        emit("V", lambda: g.vector.tensor_tensor(out, a, b, op), r, w)
+
+    def cpy(out, a, r, w):
+        emit("V", lambda: g.vector.tensor_copy(out, a), r, w)
+
+    def mmul(out, l, rhs, start, stop, r, w):
+        emit("P", lambda: g.tensor.matmul(out, l, rhs, start, stop), r, w, accum=not start)
+
+    def act(out, a, f, r, w, **kw):
+        emit("S", lambda: g.scalar.activation(out, a, f, **kw), r, w)
+
+    xs = [T.xa, T.xc]
+    hs = [slice(0, H), slice(H, P)]
+
+    dma("Y", T.xi[:, 0:H], T.x0[:, 0:H], [], ["xi0"])
+    dma("S", T.xi[:, H:P], T.x0[:, H:P], [], ["xi1"])
+    dma("Y", T.ni[:], T.nb[:], [], ["ni"])
+    dma("S", T.di[:], T.dice[:], [], ["di"])
+    dma("Y", T.ri[:], T.res[:], [], ["ri"])
+
+    emit("G", lambda: g.iota(T.t2[:], [[-16, 8], [0, 16]], 0, 1), [], ["t2"])
+    emit("G", lambda: g.iota(T.t1[:], [[-1, 128]], 0, 1), [], ["t1"])
+    emit("G", lambda: g.iota(T.vvc[:], [[16, 64]], 0, 0, allow_small_or_imprecise_dtypes=True), [], ["vvc"])
+    emit("G", lambda: g.iota(T.t5[:], [[1, 8], [0, 16]], 0, -1), [], ["t5"])
+    emit("G", lambda: g.iota(T.lo[:], [[0, 16], [1, 64]], 0, 0, allow_small_or_imprecise_dtypes=True), [], ["lo"])
+    emit("G", lambda: g.iota(T.dat[:], [[1, 16], [0, 64]], 16 * q, 0, allow_small_or_imprecise_dtypes=True), [], ["dat"])
+    emit("V", lambda: g.vector.memset(T.bp[:], 0.0), [], ["bp"])
+    emit("V", lambda: g.vector.memset(T.z64[:], 0.0), [], ["z64"])
+    ts(T.t2s[:], T.t2[:], 4, A.arith_shift_right, ["t2"], ["t2s"])
+    ts(T.t3[:], T.t1[:, 0:16], 15, A.bitwise_and, ["t1"], ["t3"])
+    ts(T.mb[:], T.t2s[:], 0, A.is_equal, ["t2s"], ["mb"])
+    ts(T.r16[:], T.t3[:], 0, A.is_equal, ["t3"], ["r16"], 256.0, A.mult)
+    cpy(T.bp[:, 16:144:16], T.mb[:, 0:128:16], ["mb"], ["bp"])
+    ts(T.idn[:], T.t1[:], 0, A.is_equal, ["t1"], ["idn"])
+    NS = 10
+    for i in range(NS):
+        e = T.ex[:, i * 128:(i + 1) * 128]
+        act(e, T.mb[:], F.Copy, ["mb", "r16"], [("ex", i)], scale=T.r16[:, i:i + 1])
+    for i in range(NS, 16):
+        ts(T.ex[:, i * 128:(i + 1) * 128], T.mb[:], T.r16[:, i:i + 1], A.mult, ["mb", "r16"], [("ex", i)])
+    for h in (0, 1):
+        cpy(T.xa[:, hs[h]], T.xi[:, hs[h]], ["xi%d" % h], [("x", 0, h)])
+    ts(T.su1[:], T.t1[:], 0, A.is_gt, ["t1"], ["su1"], -1.0, A.mult)
+    ts(T.i2[:], T.t1[:], 0, A.is_equal, ["t1"], ["i2"], -2048.0, A.mult)
+    tt(T.su[:], T.su1[:], T.mb[:], A.mult, ["su1", "mb"], ["su"])
+    tt(T.su2[:], T.su[:], T.i2[:], A.add, ["su", "i2"], ["su2"])
+    dma("Y", T.dat[1:128:16, :], T.lo[0:8, :], ["lo"], ["dat"])
+
+    def total(t):
+        x = xs[t % 2]
+        for i in range(16):
+            mmul(T.tc[:, 0:64], T.bp[:, 16 - i:144 - i], x[:, i:P:16], i == 0, i == 15,
+                 ["bp", ("x", t % 2, 0), ("x", t % 2, 1)], ["tc"])
+
+    def flag(t, late):
+        x = xs[t % 2]
+        tc = T.tc
+        ts(T.high[:], tc[:, 0:64], float(TH), A.is_ge, ["tc"], ["high"])
+        for n, l in ((1, "mb"), (2, "su2"), (3, "su")):
+            mmul(tc[:, 64 * n:64 * n + 64], T[l][:], T.high[:], True, True, [l, "high"], ["tc"])
+        for h in (0, 1):
+            mmul(T["e%d" % h][:], T.idn[:], x[:, hs[h]], True, False, ["idn", ("x", t % 2, h)], ["e%d" % h])
+        emit("V", lambda: g.vector.tensor_tensor_scan(T.pre[:], tc[:, 64:128], T.z64[:], 0.0, A.add, A.add),
+             ["tc", "z64"], ["pre"])
+        late()
+        tt(T.zz[:], T.pre[:], tc[:, 128:192], A.add, ["pre", "tc"], ["zz"])
+        ts(T.ill[:], T.zz[:], CAP - 2048 + 0.5, A.is_le, ["zz"], ["ill"])
+        w = T["win%d" % t]
+        for h in (0, 1):
+            e = T["e%d" % h]
+            for i in range(16):
+                mmul(e[:, i:H:16], T.ex[:, i * 128:(i + 1) * 128], T.ill[:, 32 * h:32 * h + 32], False, i == 15,
+                     [("ex", i), "ill"], ["e%d" % h])
+            o = w[:, q * P + h * H:q * P + (h + 1) * H]
+            if h == 0:
+                ts(o, e[:], -256.0, A.add, ["e0"], [("win", t, 0)], 0.0, A.max)
+            else:
+                act(o, e[:], F.Relu, ["e1"], [("win", t, 1)], bias=-256.0)
+        seg = w[:, q * P:(q + 1) * P]
+        send(seg, seg, "al%d" % t, [("win", t, 0), ("win", t, 1)])
+        m = T.cw[:, t:t + 1]
+        ts(m, T.pre[:, 63:64], float(CAP), A.min, ["pre"], [("cw", t)])
+        send(T.cnt[:, 4 * t + q:4 * t + q + 1], m, "ac%d" % t, [("cw", t)])
+
+    def scatter(t):
+        if t == 0:
+            ts(T.pmi[:], T.t1[:, 0:1], 15, A.bitwise_and, ["t1"], ["pmi"])
+            cpy(T.pmf[:, 0:1], T.pmi[:], ["pmi"], ["pmf"])
+            ts(T.vv[:], T.vvc[:], T.pmf[:, 0:1], A.add, ["vvc", "pmf"], ["vv"])
+        m = T.cw[:, t:t + 1]
+        right = q % 2 == 0
+        tt(T.cum[:], T.pre[:], T.tc[:, 192:256], A.add, ["pre", "tc"], ["cum"])
+        ts(T.ee[:], T.zz[:], CAP - 2048 + 0.5, A.is_gt if right else A.is_le, ["zz"], ["ee"], float(P), A.mult)
+        ts(T.cum[:], T.cum[:], float(CAP), A.min, ["cum"], ["cum"])
+        tt(T.ee[:], T.ee[:], T.vv[:], A.min if right else A.max, ["ee", "vv"], ["ee"])
+        tt(T.pos[:], T.ee[:], T.cum[:], A.subtract, ["ee", "cum"], ["pos"])
+        if right:
+            ts(T.pos16[:], T.pos[:], m, A.add, ["pos", ("cw", t)], ["pos16"])
+        else:
+            cpy(T.pos16[:], T.pos[:], ["pos"], ["pos16"])
+        seg = T["sw%d" % t][:, q * P:(q + 1) * P]
+        emit("V", lambda: g.vector.tensor_copy(seg.indirect(T.pos16[:, 0:64]), T.dat[:]), ["pos16", "dat"], [("sw", t, "own")])
+        send(seg, seg, "as%d" % t, [("sw", t, "own")])
+
+    def places(t):
+        c = [T.cw[:, t:t + 1] if r == q else T.cnt[:, 4 * t + r:4 * t + r + 1] for r in range(4)]
+        rd = [("cw", t), ("cnt", t)]
+        k = T.col
+        tt(k[:, 0:1], c[1], c[2], A.add, rd, ["k0"])
+        tt(k[:, 1:2], c[0], c[3], A.add, rd, ["k1"])
+        ts(k[:, 3:4], c[0], -0.5 + EPS, A.add, rd, ["k3"])
+        ts(k[:, 4:5], c[1], -1.0, A.mult, rd, ["k4"], 2047.5, A.add)
+        tt(k[:, 1:2], k[:, 0:1], k[:, 1:2], A.add, ["k0", "k1"], ["k1"])
+        ts(k[:, 2:3], k[:, 1:2], -1.0 / 2048, A.mult, ["k1"], ["k2"], 2.0, A.add)
+        d, dk = (T.di, "di") if t == 0 else (T["dd%d" % t], ("dd", t))
+        ts(T.yy[:], d[:], k[:, 2:3], A.mult, [dk, "k2", "k3"], ["yy"], k[:, 3:4], A.add)
+        ts(T.hh[:], T.yy[:], k[:, 4:5], A.is_ge, ["yy", "k4", "k0"], ["hh"], k[:, 0:1], A.mult)
+        tt(T.oi[:], T.yy[:], T.hh[:], A.add, ["yy", "hh"], ["oi"])
+        cpy(T.offs[:], T.oi[:], ["oi"], ["offs"])
+
+    def draws(t):
+        ts(T.dtmp[:], T.di[:], STEP * t, A.add, ["di"], ["dtmp"])
+        ts(T["dd%d" % t][:], T.dtmp[:], M2, A.bitwise_and, ["dtmp"], [("dd", t)])
+
+    def sums(bank, key, lhs, src, srck, k, i0, i1, first, last, extra=None):
+        o = bank[:, 64 * k:64 * k + 64]
+        for i in range(i0, i1):
+            mmul(o, lhs[0][:, 16 - i:144 - i], src[:, k * P + i:(k + 1) * P:16], first and i == i0,
+                 last and extra is None and i == i1 - 1, [lhs[1], (srck, k, 0), (srck, k, 1)], [key])
+        if extra is not None:
+            l, lk, rhs, rk = extra
+            mmul(o, l[:], rhs, False, True, [lk, rk], [key])
+
+    def hits(k, i0=0, i1=16):
+        sums(T.ht, "ht", (T.bp, "bp"), T.raw, "raw", k, i0, i1, i0 == 0, i1 == 16,
+             (T.ineg, "ineg", T.ill[:], "ill") if i1 == 16 else None)
+
+    def slsum(k):
+        sums(T.sl, "sl", (T.cp, "cp"), T.rsl, "rsl", k, 0, 16, True, True,
+             (T.ihalf, "ihalf", T.h2[:, 64 * k:64 * k + 64], "h2"))
+
+    def fetch(qn, win, wk, offs, ok, out, outk, k, h):
+        o = out[:, k * P + h * H:k * P + (h + 1) * H]
+        s = win[:].indirect(offs[:, 64 * k + 32 * h:64 * k + 32 * h + 32])
+        if qn == "V":
+            cpy(o, s, wk + [ok], [(outk, k, h)])
+        else:
+            act(o, s, F.Copy, wk + [ok], [(outk, k, h)])
+
+    def loads(t):
+        w = T["win%d" % t]
+        wk = [("win", t, 0), ("win", t, 1), ("win", t, "rem")]
+        nx = (t + 1) % 2
+        last = t == DAYS - 1
+        for h in (0, 1):
+            fetch("V", w, wk, T.off, "off", T.raw, "raw", 0, h)
+        for k in (1, 2, 3):
+            for h in (0, 1):
+                fetch("S", w, wk, T.off, "off", T.raw, "raw", k, h)
+        banks = ["c0", "c1", "c2"]
+        nb = [0]
+
+        def lift(k, h):
+            b = banks[nb[0] % 3]
+            nb[0] += 1
+            mmul(T[b][:], T.idn[:], T.raw[:, k * P + h * H:k * P + (h + 1) * H], True, True, ["idn", ("raw", k, h)], [b])
+            return b
+
+        def most(k, h, b):
+            a = T.raw[:, hs[h]] if k == 1 else T.mm[:, hs[h]]
+            tt(T.mm[:, hs[h]], a, T[b][:], A.max, [("raw", 0, h) if k == 1 else ("mm", h), b], [("mm", h)])
+
+        def resist(h):
+            mmul(T["e%d" % h][:], T.er[:], T.rneg[:, hs[h]], True, False, ["er", "rneg"], ["e%d" % h])
+
+        def less(h):
+            mmul(T["e%d" % h][:], T.idn[:], T.mm[:, hs[h]], False, True, ["idn", ("mm", h)], ["e%d" % h])
+
+        def newx(h):
+            o = T.yo if last else xs[nx]
+            tt(o[:, hs[h]], T.xm[:, hs[h]], T["e%d" % h][:], A.max, ["xm", "e%d" % h], [("yo", h) if last else ("x", nx, h)])
+            if last:
+                dma("Y", T.yx[:, hs[h]], T.yo[:, hs[h]], [("yo", h)], [("yx", h)])
+
+        b = lift(1, 0)
+        most(1, 0, b)
+        b = lift(1, 1)
+        most(1, 1, b)
+        hits(0)
+        places(t)
+        b = lift(2, 0)
+        most(2, 0, b)
+        b = lift(2, 1)
+        most(2, 1, b)
+        hits(1)
+        b = lift(3, 0)
+        most(3, 0, b)
+        resist(0)
+        hits(2, 0, 8)
+        less(0)
+        newx(0)
+        b = lift(3, 1)
+        most(3, 1, b)
+        resist(1)
+        hits(2, 8, 16)
+        less(1)
+        hits(3, 0, 8)
+        newx(1)
+
+    def struck():
+        ts(T.h2[:], T.ht[:, 0:256], 0.0, A.is_gt, ["ht"], ["h2"], -2 * SH, A.mult)
+
+    def keep():
+        tt(T.lk[:], T.ll[:], T.h2[:], A.add, ["ll", "h2"], ["lk"])
+
+    swk = [[("sw", t, "own"), ("sw", t, "rem")] for t in range(DAYS)]
+
+    def slfetch(qn, t, k, h):
+        fetch(qn, T["sw%d" % t], swk[t], T.offs, "offs", T.rsl, "rsl", k, h)
+
+    total(0)
+    flag(0, lambda: None)
+    scatter(0)
+    cpy(T.off[:], T.ni[:], ["ni"], ["off"])
+    x = xs[0]
+    ts(T.xm[:], x[:], -8.0, A.add, [("x", 0, 0), ("x", 0, 1)], ["xm"], 0.0, A.max)
+    ts(T.rneg[:], T.ri[:], -1.0, A.mult, ["ri"], ["rneg"])
+    ts(T.er[:], T.t5[:], 0, A.is_equal, ["t5"], ["er"])
+    ts(T.ineg[:], T.t1[:], 0, A.is_equal, ["t1"], ["ineg"], -SH, A.mult)
+    ts(T.ihalf[:], T.t1[:], 0, A.is_equal, ["t1"], ["ihalf"], -0.5, A.mult)
+    ts(T.pmf[:, 1:2], T.pmi[:], 0, A.is_equal, ["pmi"], ["pmf1"], 64.0, A.mult)
+    ts(T.pmf[:, 2:3], T.pmi[:], 1, A.is_equal, ["pmi"], ["pmf2"])
+    tt(T.pmf[:, 3:4], T.pmf[:, 1:2], T.pmf[:, 2:3], A.add, ["pmf1", "pmf2"], ["pmf3"])
+    ts(T.cp[:], T.bp[:], T.pmf[:, 3:4], A.mult, ["bp", "pmf3"], ["cp"])
+    ts(T.ll[:], T.ni[:], SH, A.add, ["ni"], ["ll"])
+
+    for t in range(DAYS):
+        loads(t)
+        if t == DAYS - 1:
+            break
+        draws(t + 1)
+        for k in (0, 1):
+            for h in (0, 1):
+                slfetch("S", t, k, h)
+        total(t + 1)
+        flag(t + 1, lambda: (hits(3, 8, 16), struck()))
+        scatter(t + 1)
+        for k in (2, 3):
+            for h in (0, 1):
+                slfetch("S", t, k, h)
+        keep()
+        for k in range(4):
+            slsum(k)
+        ts(T.xm[:], xs[(t + 1) % 2][:], -8.0, A.add, [("x", (t + 1) % 2, 0), ("x", (t + 1) % 2, 1)], ["xm"], 0.0, A.max)
+        tt(T.ll[:], T.lk[:], T.sl[:, 0:256], A.max, ["lk", "sl"], ["ll"])
+        ts(T.off[:], T.ll[:], -SH, A.add, ["ll"], ["off"])
+
+    t = DAYS - 1
+    hits(3, 8, 16)
+    struck()
+    keep()
+    for k, h in ((0, 0), (0, 1), (1, 0), (1, 1), (2, 0)):
+        slfetch("S", t, k, h)
+    for k, h in ((3, 0), (3, 1), (2, 1)):
+        slfetch("V", t, k, h)
+    for k in (0, 1, 3, 2):
+        slsum(k)
+    tt(T.ll[:], T.lk[:], T.sl[:, 0:256], A.max, ["lk", "sl"], ["ll"])
+    ts(T.no[:], T.ll[:], -SH, A.add, ["ll"], ["no"])
+    dma("Y", T.ynb[:], T.no[:], ["no"], ["ynb"])
+
+    sync_to("G", [lastw["ynb"], lastw[("yx", 0)], lastw[("yx", 1)]])
+    for k in ("V", "S", "P", "G"):
+        g.wait_ge(T.sem[psem[k]], done[k])
+    g.wait_ge(T.sem.sent, nsent[0])

@@ -1,40 +1,46 @@
 from concourse.bass import DstId, RemoteDMATransfer
-from concourse.mybir import AluOpType as A, AxisListType, ActivationFunctionType as F
+from concourse.mybir import AluOpType as A, ActivationFunctionType as F
 
 DAYS, P, CAP, TH, STEP, M2 = 4, 1024, 384, 1200, 77, 2047
 H = 512
+VG = ((0, 0), (0, 1))
+SG = ((1, 0), (1, 1), (2, 0), (2, 1), (3, 0), (3, 1))
+PRE, POST = ((0, 0), (0, 1), (1, 0)), ((1, 1), (2, 0), (2, 1), (3, 0), (3, 1))
 EPS = 2.0 ** -12
 SH = 8192.0
-SCRATCH = {
-    "xi": ("sbuf", [128, P], "int32"), "ni": ("sbuf", [128, 256], "int32"), "di": ("sbuf", [128, 256], "int32"),
-    "dtmp": ("sbuf", [128, 256], "int32"), "ri": ("sbuf", [8, P], "int32"), "rneg": ("sbuf", [8, P], "bfloat16"),
-    "xa": ("sbuf", [128, P], "bfloat16"), "xc": ("sbuf", [128, P], "bfloat16"), "xm": ("sbuf", [128, P], "bfloat16"),
-    "mm": ("sbuf", [128, P], "bfloat16"), "raw": ("sbuf", [128, 4 * P], "bfloat16"), "rsl": ("sbuf", [128, 4 * P], "bfloat16"),
-    "yo": ("sbuf", [128, P], "float32"), "no": ("sbuf", [128, 256], "float32"),
-    "off": ("sbuf", [128, 256], "uint16"), "offs": ("sbuf", [128, 256], "uint16"), "pos16": ("sbuf", [128, 64], "uint16"),
-    "ll": ("sbuf", [128, 256], "float32"), "lk": ("sbuf", [128, 256], "float32"), "h2": ("sbuf", [128, 256], "bfloat16"),
-    "yy": ("sbuf", [128, 256], "float32"), "hh": ("sbuf", [128, 256], "float32"), "oi": ("sbuf", [128, 256], "int32"),
-    "high": ("sbuf", [128, 64], "bfloat16"), "ill": ("sbuf", [128, 64], "bfloat16"), "pre": ("sbuf", [128, 64], "float32"),
-    "zz": ("sbuf", [128, 64], "float32"), "cum": ("sbuf", [128, 64], "float32"), "ee": ("sbuf", [128, 64], "float32"),
-    "pos": ("sbuf", [128, 64], "float32"), "z64": ("sbuf", [128, 64], "float32"), "vvc": ("sbuf", [128, 64], "float32"),
-    "vv": ("sbuf", [128, 64], "float32"), "cw": ("sbuf", [128, 4], "float32"), "cnt": ("sbuf", [128, 16], "float32"),
-    "col": ("sbuf", [128, 16], "float32"), "pmi": ("sbuf", [128, 1], "int32"), "pmf": ("sbuf", [128, 4], "float32"),
-    "t1": ("sbuf", [128, 128], "int32"), "t2": ("sbuf", [128, 128], "int32"), "t2s": ("sbuf", [128, 128], "int32"),
-    "t3": ("sbuf", [128, 16], "int32"), "r16": ("sbuf", [128, 16], "float32"), "t5": ("sbuf", [8, 128], "int32"),
-    "er": ("sbuf", [8, 128], "bfloat16"), "mb": ("sbuf", [128, 128], "bfloat16"), "idn": ("sbuf", [128, 128], "bfloat16"),
-    "ineg": ("sbuf", [128, 128], "bfloat16"), "ihalf": ("sbuf", [128, 128], "bfloat16"), "su": ("sbuf", [128, 128], "bfloat16"),
-    "su1": ("sbuf", [128, 128], "bfloat16"), "i2": ("sbuf", [128, 128], "bfloat16"), "su2": ("sbuf", [128, 128], "bfloat16"),
-    "bp": ("sbuf", [128, 144], "bfloat16"), "cp": ("sbuf", [128, 144], "bfloat16"), "ex": ("sbuf", [128, 2048], "bfloat16"),
-    "dat": ("sbuf", [128, P], "bfloat16"), "lo": ("sbuf", [8, P], "bfloat16"),
-}
-for _t in range(DAYS):
-    SCRATCH["win%d" % _t] = ("sbuf", [128, 4 * P], "bfloat16")
-    SCRATCH["sw%d" % _t] = ("sbuf", [128, 4 * P], "bfloat16")
-for _t in range(1, DAYS):
-    SCRATCH["dd%d" % _t] = ("sbuf", [128, 256], "int32")
+
+
+def _sb(dtype, *names, cols, rows=128):
+    return {n: ("sbuf", [rows, cols], dtype) for n in names}
+
+
+SCRATCH = {}
+SCRATCH.update(_sb("int32", "xi", cols=P))
+SCRATCH.update(_sb("int32", "ni", "di", "dtmp", "oi", "dd1", "dd2", "dd3", cols=256))
+SCRATCH.update(_sb("int32", "t1", "t2", "t2s", cols=128))
+SCRATCH.update(_sb("int32", "ri", cols=64))
+SCRATCH.update(_sb("int32", "t3", cols=16))
+SCRATCH.update(_sb("int32", "pmi", cols=1))
+SCRATCH.update(_sb("uint16", "off", "offs0", "offs1", cols=256))
+SCRATCH.update(_sb("uint16", "pos16", cols=64))
+SCRATCH.update(_sb("bfloat16", "xa", "xc", "xm", "mm", "dat", cols=P))
+SCRATCH.update(_sb("bfloat16", "raw", "rsl", cols=4 * P))
+SCRATCH.update(_sb("bfloat16", *["win%d" % _t for _t in range(DAYS)], *["sw%d" % _t for _t in range(DAYS)], cols=4 * P))
+SCRATCH.update(_sb("bfloat16", "rneg", "lo", cols=P, rows=8))
+SCRATCH.update(_sb("bfloat16", "er", cols=128, rows=8))
+SCRATCH.update(_sb("bfloat16", "ex", cols=2048))
+SCRATCH.update(_sb("bfloat16", "sg", cols=256))
+SCRATCH.update(_sb("bfloat16", "bp", "cp", cols=144))
+SCRATCH.update(_sb("bfloat16", "mb", "idn", "id2", "id3", "id4", "ineg", "su", "su1", "i2", "su2", cols=128))
+SCRATCH.update(_sb("bfloat16", "high", "ill0", "ill1", "rw", cols=64))
+SCRATCH.update(_sb("float32", "yo", cols=P))
+SCRATCH.update(_sb("float32", "no", "ll", "lk", "hh", cols=256))
+SCRATCH.update(_sb("float32", "pre", "zz", "cum", "ee", "pos", "z64", "vvc", "vv", "sel", cols=64))
+SCRATCH.update(_sb("float32", "cnt", "col", "r16", cols=16))
+SCRATCH.update(_sb("float32", "cw", "pmf", cols=4))
 for _b in ("c0", "c1", "c2", "e0", "e1", "ht", "sl", "tc"):
     SCRATCH[_b] = ("psum", [128, 512], "float32")
-SEMAPHORES = ["pv", "ps", "pp", "pg", "sent"] + ["dm%d" % i for i in range(12)]
+SEMAPHORES = ["pv", "ps", "pp", "pg", "sent"] + ["dm%d" % i for i in range(14)]
 SEMAPHORES += [k + "%d" % t for k in ("al", "ac", "as") for t in range(DAYS)]
 
 
@@ -60,6 +66,7 @@ def rank_program(g, core, T, topo):
     if q is None:
         return
     cores = list(T.cores)
+    right = q % 2 == 0
     eng = {c: plan(topo, cores, c) for c in cores}
     queue = {"V": g.vector, "S": g.scalar, "P": g.tensor, "G": g, "Y": g.sync}
     psem = {"V": "pv", "S": "ps", "P": "pp", "G": "pg"}
@@ -93,7 +100,7 @@ def rank_program(g, core, T, topo):
         for k in writes:
             if k in lastw and not (accum and lastw[k][3] == qn):
                 toks.append(lastw[k])
-            toks += [t for t in readers.get(k, []) if t[3] != qn]
+            toks += readers.get(k, [])
         sync_to(qn, toks)
 
     def record(tok, reads, writes):
@@ -115,9 +122,7 @@ def rank_program(g, core, T, topo):
         s = "dm%d" % ndma[0]
         ndma[0] += 1
         queue[qn].dma_start(out, in_).then_inc(T.sem[s], 16)
-        tok = (s, 16, dict(known[qn]), None)
-        record(tok, reads, writes)
-        return tok
+        record((s, 16, dict(known[qn]), None), reads, writes)
 
     def send(dst_ap, src_ap, sem, reads):
         deps("G", reads, [], False)
@@ -157,10 +162,12 @@ def rank_program(g, core, T, topo):
         emit("S", lambda: g.scalar.activation(out, a, f, **kw), r, w)
 
     xs = [T.xa, T.xc]
+    ills = [T.ill0, T.ill1]
     hs = [slice(0, H), slice(H, P)]
+    qs = [slice(n * 256, n * 256 + 256) for n in range(4)]
 
-    dma("Y", T.xi[:, 0:H], T.x0[:, 0:H], [], ["xi0"])
-    dma("S", T.xi[:, H:P], T.x0[:, H:P], [], ["xi1"])
+    for n in range(4):
+        dma("YS"[n % 2], T.xi[:, qs[n]], T.x0[:, qs[n]], [], [("xi", n)])
     dma("Y", T.ni[:], T.nb[:], [], ["ni"])
     dma("S", T.di[:], T.dice[:], [], ["di"])
     dma("Y", T.ri[:], T.res[:], [], ["ri"])
@@ -168,7 +175,6 @@ def rank_program(g, core, T, topo):
     emit("G", lambda: g.iota(T.t2[:], [[-16, 8], [0, 16]], 0, 1), [], ["t2"])
     emit("G", lambda: g.iota(T.t1[:], [[-1, 128]], 0, 1), [], ["t1"])
     emit("G", lambda: g.iota(T.vvc[:], [[16, 64]], 0, 0, allow_small_or_imprecise_dtypes=True), [], ["vvc"])
-    emit("G", lambda: g.iota(T.t5[:], [[1, 8], [0, 16]], 0, -1), [], ["t5"])
     emit("G", lambda: g.iota(T.lo[:], [[0, 16], [1, 64]], 0, 0, allow_small_or_imprecise_dtypes=True), [], ["lo"])
     emit("G", lambda: g.iota(T.dat[:], [[1, 16], [0, 64]], 16 * q, 0, allow_small_or_imprecise_dtypes=True), [], ["dat"])
     emit("V", lambda: g.vector.memset(T.bp[:], 0.0), [], ["bp"])
@@ -178,20 +184,19 @@ def rank_program(g, core, T, topo):
     ts(T.mb[:], T.t2s[:], 0, A.is_equal, ["t2s"], ["mb"])
     ts(T.r16[:], T.t3[:], 0, A.is_equal, ["t3"], ["r16"], 256.0, A.mult)
     cpy(T.bp[:, 16:144:16], T.mb[:, 0:128:16], ["mb"], ["bp"])
+    for i in range(16):
+        act(T.ex[:, i * 128:(i + 1) * 128], T.mb[:], F.Copy, ["mb", "r16"], [("ex", i)], scale=T.r16[:, i:i + 1])
     ts(T.idn[:], T.t1[:], 0, A.is_equal, ["t1"], ["idn"])
-    NS = 10
-    for i in range(NS):
-        e = T.ex[:, i * 128:(i + 1) * 128]
-        act(e, T.mb[:], F.Copy, ["mb", "r16"], [("ex", i)], scale=T.r16[:, i:i + 1])
-    for i in range(NS, 16):
-        ts(T.ex[:, i * 128:(i + 1) * 128], T.mb[:], T.r16[:, i:i + 1], A.mult, ["mb", "r16"], [("ex", i)])
-    for h in (0, 1):
-        cpy(T.xa[:, hs[h]], T.xi[:, hs[h]], ["xi%d" % h], [("x", 0, h)])
     ts(T.su1[:], T.t1[:], 0, A.is_gt, ["t1"], ["su1"], -1.0, A.mult)
     ts(T.i2[:], T.t1[:], 0, A.is_equal, ["t1"], ["i2"], -2048.0, A.mult)
     tt(T.su[:], T.su1[:], T.mb[:], A.mult, ["su1", "mb"], ["su"])
+    for n in range(4):
+        cpy(T.xa[:, qs[n]], T.xi[:, qs[n]], [("xi", n)], [("x", 0, n // 2)])
     tt(T.su2[:], T.su[:], T.i2[:], A.add, ["su", "i2"], ["su2"])
+    ts(T.rw[:], T.ri[:], -1.0, A.mult, ["ri"], ["rw"])
     dma("Y", T.dat[1:128:16, :], T.lo[0:8, :], ["lo"], ["dat"])
+    dma("Y", T.er[0:8, :], T.mb[0:128:16, :], ["mb"], ["er"])
+    dma("Y", T.rneg[0:8, :], T.rw[:], ["rw"], ["rneg"])
 
     def total(t):
         x = xs[t % 2]
@@ -199,9 +204,10 @@ def rank_program(g, core, T, topo):
             mmul(T.tc[:, 0:64], T.bp[:, 16 - i:144 - i], x[:, i:P:16], i == 0, i == 15,
                  ["bp", ("x", t % 2, 0), ("x", t % 2, 1)], ["tc"])
 
-    def flag(t, late):
+    def flag(t, between):
         x = xs[t % 2]
         tc = T.tc
+        ill, illk = ills[t % 2], ("ill", t % 2)
         ts(T.high[:], tc[:, 0:64], float(TH), A.is_ge, ["tc"], ["high"])
         for n, l in ((1, "mb"), (2, "su2"), (3, "su")):
             mmul(tc[:, 64 * n:64 * n + 64], T[l][:], T.high[:], True, True, [l, "high"], ["tc"])
@@ -209,15 +215,20 @@ def rank_program(g, core, T, topo):
             mmul(T["e%d" % h][:], T.idn[:], x[:, hs[h]], True, False, ["idn", ("x", t % 2, h)], ["e%d" % h])
         emit("V", lambda: g.vector.tensor_tensor_scan(T.pre[:], tc[:, 64:128], T.z64[:], 0.0, A.add, A.add),
              ["tc", "z64"], ["pre"])
-        late()
+        act(T.cw[:, t:t + 1], T.pre[:, 63:64], F.Relu, ["pre"], [("cw", t)], scale=-1.0, bias=float(CAP))
         tt(T.zz[:], T.pre[:], tc[:, 128:192], A.add, ["pre", "tc"], ["zz"])
-        ts(T.ill[:], T.zz[:], CAP - 2048 + 0.5, A.is_le, ["zz"], ["ill"])
+        ts(ill[:], T.zz[:], CAP - 2048 + 0.5, A.is_le, ["zz"], [illk])
+        between()
+        if right:
+            act(T.sel[:], ill[:], F.Copy, [illk], ["sel"], scale=-float(P), bias=float(P))
+        else:
+            act(T.sel[:], ill[:], F.Copy, [illk], ["sel"], scale=float(P))
         w = T["win%d" % t]
         for h in (0, 1):
             e = T["e%d" % h]
             for i in range(16):
-                mmul(e[:, i:H:16], T.ex[:, i * 128:(i + 1) * 128], T.ill[:, 32 * h:32 * h + 32], False, i == 15,
-                     [("ex", i), "ill"], ["e%d" % h])
+                mmul(e[:, i:H:16], T.ex[:, i * 128:(i + 1) * 128], ill[:, 32 * h:32 * h + 32], False, i == 15,
+                     [("ex", i), illk], ["e%d" % h])
             o = w[:, q * P + h * H:q * P + (h + 1) * H]
             if h == 0:
                 ts(o, e[:], -256.0, A.add, ["e0"], [("win", t, 0)], 0.0, A.max)
@@ -225,66 +236,67 @@ def rank_program(g, core, T, topo):
                 act(o, e[:], F.Relu, ["e1"], [("win", t, 1)], bias=-256.0)
         seg = w[:, q * P:(q + 1) * P]
         send(seg, seg, "al%d" % t, [("win", t, 0), ("win", t, 1)])
-        m = T.cw[:, t:t + 1]
-        ts(m, T.pre[:, 63:64], float(CAP), A.min, ["pre"], [("cw", t)])
-        send(T.cnt[:, 4 * t + q:4 * t + q + 1], m, "ac%d" % t, [("cw", t)])
+        send(T.cnt[:, 4 * t + q:4 * t + q + 1], T.cw[:, t:t + 1], "ac%d" % t, [("cw", t)])
 
     def scatter(t):
-        if t == 0:
-            ts(T.pmi[:], T.t1[:, 0:1], 15, A.bitwise_and, ["t1"], ["pmi"])
-            cpy(T.pmf[:, 0:1], T.pmi[:], ["pmi"], ["pmf"])
-            ts(T.vv[:], T.vvc[:], T.pmf[:, 0:1], A.add, ["vvc", "pmf"], ["vv"])
-        m = T.cw[:, t:t + 1]
-        right = q % 2 == 0
         tt(T.cum[:], T.pre[:], T.tc[:, 192:256], A.add, ["pre", "tc"], ["cum"])
-        ts(T.ee[:], T.zz[:], CAP - 2048 + 0.5, A.is_gt if right else A.is_le, ["zz"], ["ee"], float(P), A.mult)
-        ts(T.cum[:], T.cum[:], float(CAP), A.min, ["cum"], ["cum"])
-        tt(T.ee[:], T.ee[:], T.vv[:], A.min if right else A.max, ["ee", "vv"], ["ee"])
+        if right:
+            ts(T.cum[:], T.cum[:], float(CAP), A.min, ["cum"], ["cum"], -float(CAP), A.add)
+        else:
+            ts(T.cum[:], T.cum[:], float(CAP), A.min, ["cum"], ["cum"])
+        tt(T.ee[:], T.sel[:], T.vv[:], A.min if right else A.max, ["sel", "vv"], ["ee"])
         tt(T.pos[:], T.ee[:], T.cum[:], A.subtract, ["ee", "cum"], ["pos"])
         if right:
-            ts(T.pos16[:], T.pos[:], m, A.add, ["pos", ("cw", t)], ["pos16"])
+            ts(T.pos16[:], T.pos[:], T.cw[:, t:t + 1], A.subtract, ["pos", ("cw", t)], ["pos16"])
         else:
             cpy(T.pos16[:], T.pos[:], ["pos"], ["pos16"])
         seg = T["sw%d" % t][:, q * P:(q + 1) * P]
         emit("V", lambda: g.vector.tensor_copy(seg.indirect(T.pos16[:, 0:64]), T.dat[:]), ["pos16", "dat"], [("sw", t, "own")])
         send(seg, seg, "as%d" % t, [("sw", t, "own")])
 
-    def places(t):
+    def columns(t):
         c = [T.cw[:, t:t + 1] if r == q else T.cnt[:, 4 * t + r:4 * t + r + 1] for r in range(4)]
         rd = [("cw", t), ("cnt", t)]
         k = T.col
-        tt(k[:, 0:1], c[1], c[2], A.add, rd, ["k0"])
-        tt(k[:, 1:2], c[0], c[3], A.add, rd, ["k1"])
-        ts(k[:, 3:4], c[0], -0.5 + EPS, A.add, rd, ["k3"])
-        ts(k[:, 4:5], c[1], -1.0, A.mult, rd, ["k4"], 2047.5, A.add)
-        tt(k[:, 1:2], k[:, 0:1], k[:, 1:2], A.add, ["k0", "k1"], ["k1"])
-        ts(k[:, 2:3], k[:, 1:2], -1.0 / 2048, A.mult, ["k1"], ["k2"], 2.0, A.add)
+        f = 1.0 / 2048
+        act(k[:, 0:1], c[0], F.Copy, rd, ["k0"], scale=f, bias=1.25)
+        act(k[:, 4:5], c[1], F.Copy, rd, ["k4"], scale=-1.0, bias=2.0 * CAP)
+        act(k[:, 6:7], c[0], F.Copy, rd, ["k6"], scale=-1.0, bias=CAP - 0.5 + EPS)
+        act(k[:, 1:2], c[1], F.Identity, rd + ["k0"], ["k1"], scale=f, bias=k[:, 0:1])
+        act(k[:, 5:6], c[2], F.Identity, rd + ["k4"], ["k5"], scale=-1.0, bias=k[:, 4:5])
+        act(k[:, 7:8], c[1], F.Copy, rd, ["k7"], bias=2047.5 - CAP)
+        act(k[:, 2:3], c[2], F.Identity, rd + ["k1"], ["k2"], scale=f, bias=k[:, 1:2])
+        act(k[:, 3:4], c[3], F.Identity, rd + ["k2"], ["k3"], scale=f, bias=k[:, 2:3])
+
+    def places(t):
+        k = T.col
+        y = T.e1[:, 0:256]
         d, dk = (T.di, "di") if t == 0 else (T["dd%d" % t], ("dd", t))
-        ts(T.yy[:], d[:], k[:, 2:3], A.mult, [dk, "k2", "k3"], ["yy"], k[:, 3:4], A.add)
-        ts(T.hh[:], T.yy[:], k[:, 4:5], A.is_ge, ["yy", "k4", "k0"], ["hh"], k[:, 0:1], A.mult)
-        tt(T.oi[:], T.yy[:], T.hh[:], A.add, ["yy", "hh"], ["oi"])
-        cpy(T.offs[:], T.oi[:], ["oi"], ["offs"])
+        ts(y, d[:], k[:, 3:4], A.mult, [dk, "k3", "k6"], ["e1"], k[:, 6:7], A.add)
+        ts(T.hh[:], y, k[:, 7:8], A.is_ge, ["e1", "k7", "k5"], ["hh"], k[:, 5:6], A.mult)
+        tt(T.oi[:], y, T.hh[:], A.add, ["e1", "hh"], ["oi"])
+        cpy(T["offs%d" % (t % 2)][:], T.oi[:], ["oi"], [("offs", t % 2)])
 
     def draws(t):
         ts(T.dtmp[:], T.di[:], STEP * t, A.add, ["di"], ["dtmp"])
         ts(T["dd%d" % t][:], T.dtmp[:], M2, A.bitwise_and, ["dtmp"], [("dd", t)])
 
-    def sums(bank, key, lhs, src, srck, k, i0, i1, first, last, extra=None):
+    def sums(bank, key, lhs, src, srck, k, i0, i1, extra):
         o = bank[:, 64 * k:64 * k + 64]
         for i in range(i0, i1):
-            mmul(o, lhs[0][:, 16 - i:144 - i], src[:, k * P + i:(k + 1) * P:16], first and i == i0,
-                 last and extra is None and i == i1 - 1, [lhs[1], (srck, k, 0), (srck, k, 1)], [key])
-        if extra is not None:
+            mmul(o, lhs[0][:, 16 - i:144 - i], src[:, k * P + i:(k + 1) * P:16], i == 0, False,
+                 [lhs[1], (srck, k, 0), (srck, k, 1)], [key])
+        if i1 == 16:
             l, lk, rhs, rk = extra
             mmul(o, l[:], rhs, False, True, [lk, rk], [key])
 
-    def hits(k, i0=0, i1=16):
-        sums(T.ht, "ht", (T.bp, "bp"), T.raw, "raw", k, i0, i1, i0 == 0, i1 == 16,
-             (T.ineg, "ineg", T.ill[:], "ill") if i1 == 16 else None)
+    def hits(t, k, i0=0, i1=16):
+        sums(T.ht, "ht", (T.bp, "bp"), T.raw, "raw", k, i0, i1, (T.ineg, "ineg", ills[t % 2][:], ("ill", t % 2)))
 
-    def slsum(k):
-        sums(T.sl, "sl", (T.cp, "cp"), T.rsl, "rsl", k, 0, 16, True, True,
-             (T.ihalf, "ihalf", T.h2[:, 64 * k:64 * k + 64], "h2"))
+    def slsum(t, k):
+        l = ("idn", "id2", "id3", "id4")[t]
+        b = "sl" if k < 2 else "c2"
+        sums(T[b], b, (T.cp, "cp"), T.rsl, "rsl", k, 0, 16, (T[l], l, T.sg[:, 64 * k:64 * k + 64], "sg"))
 
     def fetch(qn, win, wk, offs, ok, out, outk, k, h):
         o = out[:, k * P + h * H:k * P + (h + 1) * H]
@@ -299,11 +311,14 @@ def rank_program(g, core, T, topo):
         wk = [("win", t, 0), ("win", t, 1), ("win", t, "rem")]
         nx = (t + 1) % 2
         last = t == DAYS - 1
-        for h in (0, 1):
-            fetch("V", w, wk, T.off, "off", T.raw, "raw", 0, h)
-        for k in (1, 2, 3):
-            for h in (0, 1):
-                fetch("S", w, wk, T.off, "off", T.raw, "raw", k, h)
+        for n, (k, h) in enumerate(VG):
+            if n == 1 and t > 0:
+                renew(t - 1, 1)
+            fetch("V", w, wk, T.off, ("off", k // 2), T.raw, "raw", k, h)
+        for k, h in SG:
+            fetch("S", w, wk, T.off, ("off", k // 2), T.raw, "raw", k, h)
+            if (k, h) == (2, 1):
+                columns(t)
         banks = ["c0", "c1", "c2"]
         nb = [0]
 
@@ -311,9 +326,6 @@ def rank_program(g, core, T, topo):
             b = banks[nb[0] % 3]
             nb[0] += 1
             mmul(T[b][:], T.idn[:], T.raw[:, k * P + h * H:k * P + (h + 1) * H], True, True, ["idn", ("raw", k, h)], [b])
-            return b
-
-        def most(k, h, b):
             a = T.raw[:, hs[h]] if k == 1 else T.mm[:, hs[h]]
             tt(T.mm[:, hs[h]], a, T[b][:], A.max, [("raw", 0, h) if k == 1 else ("mm", h), b], [("mm", h)])
 
@@ -329,92 +341,100 @@ def rank_program(g, core, T, topo):
             if last:
                 dma("Y", T.yx[:, hs[h]], T.yo[:, hs[h]], [("yo", h)], [("yx", h)])
 
-        b = lift(1, 0)
-        most(1, 0, b)
-        b = lift(1, 1)
-        most(1, 1, b)
-        hits(0)
+        lift(1, 0)
+        lift(1, 1)
+        hits(t, 0)
+        lift(2, 0)
+        lift(2, 1)
         places(t)
-        b = lift(2, 0)
-        most(2, 0, b)
-        b = lift(2, 1)
-        most(2, 1, b)
-        hits(1)
-        b = lift(3, 0)
-        most(3, 0, b)
+        hits(t, 1)
+        lift(3, 0)
         resist(0)
-        hits(2, 0, 8)
-        less(0)
-        newx(0)
-        b = lift(3, 1)
-        most(3, 1, b)
         resist(1)
-        hits(2, 8, 16)
+        hits(t, 2, 0, 8)
+        lift(3, 1)
+        less(0)
+        hits(t, 2, 8, 16)
         less(1)
-        hits(3, 0, 8)
+        newx(0)
         newx(1)
+        hits(t, 3)
 
     def struck():
-        ts(T.h2[:], T.ht[:, 0:256], 0.0, A.is_gt, ["ht"], ["h2"], -2 * SH, A.mult)
+        act(T.sg[:], T.ht[:, 0:256], F.Sign, ["ht"], ["sg"], bias=-float(TH) / 2)
 
     def keep():
-        tt(T.lk[:], T.ll[:], T.h2[:], A.add, ["ll", "h2"], ["lk"])
+        tt(T.lk[:], T.ll[:], T.sg[:], A.subtract, [("ll", 0), ("ll", 1), "sg"], ["lk"])
 
     swk = [[("sw", t, "own"), ("sw", t, "rem")] for t in range(DAYS)]
 
     def slfetch(qn, t, k, h):
-        fetch(qn, T["sw%d" % t], swk[t], T.offs, "offs", T.rsl, "rsl", k, h)
+        fetch(qn, T["sw%d" % t], swk[t], T["offs%d" % (t % 2)], ("offs", t % 2), T.rsl, "rsl", k, h)
+
+    def renew(t, u):
+        b = ("sl", "c2")[u]
+        c = slice(128 * u, 128 * u + 128)
+        tt(T.ll[:, c], T.lk[:, c], T[b][:, c], A.max, ["lk", b], [("ll", u)])
+        if t == DAYS - 1:
+            ts(T.no[:, c], T.ll[:, c], -(t + 1.0), A.add, [("ll", u)], [("no", u)], SH, A.mult)
+        else:
+            ts(T.off[:, c], T.ll[:, c], -(t + 1.0), A.add, [("ll", u)], [("off", u)], SH, A.mult)
+
+    def fade(t):
+        ts(T.xm[:], xs[t % 2][:], -8.0, A.add, [("x", t % 2, 0), ("x", t % 2, 1)], ["xm"], 0.0, A.max)
+
+    def number():
+        ts(T.pmi[:], T.t1[:, 0:1], 15, A.bitwise_and, ["t1"], ["pmi"])
+        cpy(T.pmf[:, 0:1], T.pmi[:], ["pmi"], ["pmf"])
+        ts(T.vv[:], T.vvc[:], T.pmf[:, 0:1], A.add, ["vvc", "pmf"], ["vv"])
 
     total(0)
-    flag(0, lambda: None)
+    flag(0, number)
     scatter(0)
-    cpy(T.off[:], T.ni[:], ["ni"], ["off"])
-    x = xs[0]
-    ts(T.xm[:], x[:], -8.0, A.add, [("x", 0, 0), ("x", 0, 1)], ["xm"], 0.0, A.max)
-    ts(T.rneg[:], T.ri[:], -1.0, A.mult, ["ri"], ["rneg"])
-    ts(T.er[:], T.t5[:], 0, A.is_equal, ["t5"], ["er"])
-    ts(T.ineg[:], T.t1[:], 0, A.is_equal, ["t1"], ["ineg"], -SH, A.mult)
-    ts(T.ihalf[:], T.t1[:], 0, A.is_equal, ["t1"], ["ihalf"], -0.5, A.mult)
-    ts(T.pmf[:, 1:2], T.pmi[:], 0, A.is_equal, ["pmi"], ["pmf1"], 64.0, A.mult)
-    ts(T.pmf[:, 2:3], T.pmi[:], 1, A.is_equal, ["pmi"], ["pmf2"])
-    tt(T.pmf[:, 3:4], T.pmf[:, 1:2], T.pmf[:, 2:3], A.add, ["pmf1", "pmf2"], ["pmf3"])
-    ts(T.cp[:], T.bp[:], T.pmf[:, 3:4], A.mult, ["bp", "pmf3"], ["cp"])
-    ts(T.ll[:], T.ni[:], SH, A.add, ["ni"], ["ll"])
+    cpy(T.off[:], T.ni[:], ["ni"], [("off", 0), ("off", 1)])
+    fade(0)
+    act(T.pmf[:, 1:2], T.r16[:, 1:2], F.Copy, ["r16"], ["pmf1"], scale=1.0 / 256 / SH)
+    act(T.ineg[:], T.idn[:], F.Copy, ["idn"], ["ineg"], scale=-SH)
+    act(T.pmf[:, 2:3], T.r16[:, 0:1], F.Identity, ["r16", "pmf1"], ["pmf2"], scale=64.0 / 256 / SH, bias=T.pmf[:, 1:2])
+    for n in (2, 3, 4):
+        act(T["id%d" % n][:], T.idn[:], F.Copy, ["idn"], ["id%d" % n], scale=float(n))
+    act(T.cp[:], T.bp[:], F.Copy, ["bp", "pmf2"], ["cp"], scale=T.pmf[:, 2:3])
+    ts(T.ll[:], T.ni[:], 1.0 / SH, A.mult, ["ni"], [("ll", 0), ("ll", 1)])
+    for t in range(1, DAYS):
+        draws(t)
 
-    for t in range(DAYS):
+    for t in range(DAYS - 1):
         loads(t)
-        if t == DAYS - 1:
-            break
-        draws(t + 1)
-        for k in (0, 1):
-            for h in (0, 1):
-                slfetch("S", t, k, h)
+        for n, (k, h) in enumerate(PRE):
+            if n == 2:
+                struck()
+            slfetch("S", t, k, h)
         total(t + 1)
-        flag(t + 1, lambda: (hits(3, 8, 16), struck()))
+        fade(t + 1)
+        flag(t + 1, keep)
         scatter(t + 1)
-        for k in (2, 3):
-            for h in (0, 1):
-                slfetch("S", t, k, h)
-        keep()
+        for k, h in POST:
+            slfetch("S", t, k, h)
         for k in range(4):
-            slsum(k)
-        ts(T.xm[:], xs[(t + 1) % 2][:], -8.0, A.add, [("x", (t + 1) % 2, 0), ("x", (t + 1) % 2, 1)], ["xm"], 0.0, A.max)
-        tt(T.ll[:], T.lk[:], T.sl[:, 0:256], A.max, ["lk", "sl"], ["ll"])
-        ts(T.off[:], T.ll[:], -SH, A.add, ["ll"], ["off"])
+            slsum(t, k)
+        renew(t, 0)
 
     t = DAYS - 1
-    hits(3, 8, 16)
-    struck()
-    keep()
-    for k, h in ((0, 0), (0, 1), (1, 0), (1, 1), (2, 0)):
+    loads(t)
+    for k, h in ((0, 0), (0, 1), (1, 0)):
         slfetch("S", t, k, h)
-    for k, h in ((3, 0), (3, 1), (2, 1)):
+    struck()
+    for k, h in ((1, 1), (2, 0)):
+        slfetch("S", t, k, h)
+    for k, h in ((3, 0), (3, 1)):
         slfetch("V", t, k, h)
+    keep()
+    slfetch("V", t, 2, 1)
     for k in (0, 1, 3, 2):
-        slsum(k)
-    tt(T.ll[:], T.lk[:], T.sl[:, 0:256], A.max, ["lk", "sl"], ["ll"])
-    ts(T.no[:], T.ll[:], -SH, A.add, ["ll"], ["no"])
-    dma("Y", T.ynb[:], T.no[:], ["no"], ["ynb"])
+        slsum(t, k)
+    renew(t, 0)
+    renew(t, 1)
+    dma("Y", T.ynb[:], T.no[:], [("no", 0), ("no", 1)], ["ynb"])
 
     sync_to("G", [lastw["ynb"], lastw[("yx", 0)], lastw[("yx", 1)]])
     for k in ("V", "S", "P", "G"):

@@ -1,13 +1,20 @@
 from concourse.bass import DstId, RemoteDMATransfer
-from concourse.mybir import AluOpType as A, ActivationFunctionType as F
+from concourse.mybir import AluOpType as A, ActivationFunctionType as F, AxisListType as X
 
 DAYS, P, CAP, TH, STEP, M2 = 4, 1024, 384, 1200, 77, 2047
 H = 512
-VG = ((0, 0), (0, 1))
-SG = ((1, 0), (1, 1), (2, 0), (2, 1), (3, 0), (3, 1))
-PRE, POST = ((0, 0), (0, 1), (1, 0)), ((1, 1), (2, 0), (2, 1), (3, 0), (3, 1))
 EPS = 2.0 ** -12
 SH = 8192.0
+LQ = {"00": "V", "10": "S", "20": "S", "30": "S", "01": "S", "11": "S", "21": "S", "31": "S"}
+SQ = {"00": "S", "10": "S", "20": "S", "30": "S", "01": "S", "11": "S", "21": "S", "31": "S"}
+LQL = {"00": "S", "10": "V", "20": "V", "30": "S", "01": "S", "11": "S", "21": "S", "31": "S"}
+SQL = {"00": "S", "10": "S", "20": "S", "30": "V", "01": "S", "11": "V", "21": "V", "31": "S"}
+MQ = "VS"
+FIRST = """T0 a0 F0 T1 num D1 v0 a1 off s0 m0 F1 v1 misc Z0 Z1 s1 Z2 m1 Z3 C0 Z4 D0 Z5 C1 M"""
+DAY = """g00 g10 g20 l10 l20 p0 r0 p1 g11 r1 b0 g30 g01 n0 l11 p2 h00 T0 a0 g21 l21 p3 F0 h01 v0 g31 p4 b1 n1 s0 u0 T1 k31 m0
+ k20 a1 D1 F1 k11 D0 v1 k10 s1 k00 Z0 m1 Z1 Z2 k30 C0 k21 Z3 h1 k01 C1 S0 u1 Z4 K0 Z5 M R0 O0 S1 K1 R1 O1"""
+LAST = """g10 g30 g00 g20 p0 g11 r0 g01 l10 p1 l20 h00 p2 l11 p3 b0 p4 g31 n0 h01 g21 l21 u0 k10 k30 r1 k00 k11 k20 k01 k31 b1
+ h1 u1 k21 n1 K1 S0 K0 S1 R0 R1"""
 
 
 def _sb(dtype, *names, cols, rows=128):
@@ -16,7 +23,7 @@ def _sb(dtype, *names, cols, rows=128):
 
 SCRATCH = {}
 SCRATCH.update(_sb("int32", "xi", cols=P))
-SCRATCH.update(_sb("int32", "ni", "di", "dtmp", "oi", "dd1", "dd2", "dd3", cols=256))
+SCRATCH.update(_sb("int32", "ni", "di", "dtmp", "oi", "dd0", "dd1", "dd2", "dd3", cols=256))
 SCRATCH.update(_sb("int32", "t1", "t2", "t2s", cols=128))
 SCRATCH.update(_sb("int32", "ri", cols=64))
 SCRATCH.update(_sb("int32", "t3", cols=16))
@@ -34,14 +41,15 @@ SCRATCH.update(_sb("bfloat16", "bp", "cp", cols=144))
 SCRATCH.update(_sb("bfloat16", "mb", "idn", "id2", "id3", "id4", "ineg", "su", "su1", "i2", "su2", cols=128))
 SCRATCH.update(_sb("bfloat16", "high", "ill0", "ill1", "rw", cols=64))
 SCRATCH.update(_sb("float32", "yo", cols=P))
-SCRATCH.update(_sb("float32", "no", "ll", "lk", "hh", cols=256))
+SCRATCH.update(_sb("float32", "no", "lk", "hh", "nf", cols=256))
 SCRATCH.update(_sb("float32", "pre", "zz", "cum", "ee", "pos", "z64", "vvc", "vv", "sel", cols=64))
-SCRATCH.update(_sb("float32", "cnt", "col", "r16", cols=16))
-SCRATCH.update(_sb("float32", "cw", "pmf", cols=4))
-for _b in ("c0", "c1", "c2", "e0", "e1", "ht", "sl", "tc"):
+SCRATCH.update(_sb("float32", "cnt", cols=16 * DAYS))
+SCRATCH.update(_sb("float32", "r16", cols=16))
+SCRATCH.update(_sb("float32", "pmf", "ka", "kb", cols=4))
+for _b in ("c0", "c1", "e0", "e1", "ht", "sl", "tc0", "tc1"):
     SCRATCH[_b] = ("psum", [128, 512], "float32")
-SEMAPHORES = ["pv", "ps", "pp", "pg", "sent"] + ["dm%d" % i for i in range(14)]
-SEMAPHORES += [k + "%d" % t for k in ("al", "ac", "as") for t in range(DAYS)]
+SEMAPHORES = ["pv", "ps", "pp", "pg", "sent"] + ["dm%d" % i for i in range(16)]
+SEMAPHORES += [k + "%d" % t for k in ("al", "ah", "ac", "as") for t in range(DAYS)]
 
 
 def plan(topo, cores, src):
@@ -139,8 +147,9 @@ def rank_program(g, core, T, topo):
 
     arrive = sum(len(eng[c][core]) for c in cores if c != core)
     for t in range(DAYS):
-        lastw[("win", t, "rem")] = ("al%d" % t, arrive, {}, None)
-        lastw[("cnt", t)] = ("ac%d" % t, arrive, {}, None)
+        lastw[("win", t, 0, "rem")] = ("al%d" % t, arrive, {}, None)
+        lastw[("win", t, 1, "rem")] = ("ah%d" % t, arrive, {}, None)
+        lastw[("cnt", t, "rem")] = ("ac%d" % t, arrive, {}, None)
         lastw[("sw", t, "rem")] = ("as%d" % t, arrive, {}, None)
 
     def ts(out, in0, s1, op0, r, w, s2=None, op1=None):
@@ -164,7 +173,15 @@ def rank_program(g, core, T, topo):
     xs = [T.xa, T.xc]
     ills = [T.ill0, T.ill1]
     hs = [slice(0, H), slice(H, P)]
+    cs = [slice(0, 32), slice(32, 64)]
+    ks = [slice(0, 128), slice(128, 256)]
     qs = [slice(n * 256, n * 256 + 256) for n in range(4)]
+
+    def nat(h, k):
+        return slice(64 * k + 32 * h, 64 * k + 32 * h + 32)
+
+    def own(h, k):
+        return slice(128 * h + 32 * k, 128 * h + 32 * k + 32)
 
     for n in range(4):
         dma("YS"[n % 2], T.xi[:, qs[n]], T.x0[:, qs[n]], [], [("xi", n)])
@@ -190,251 +207,267 @@ def rank_program(g, core, T, topo):
     ts(T.su1[:], T.t1[:], 0, A.is_gt, ["t1"], ["su1"], -1.0, A.mult)
     ts(T.i2[:], T.t1[:], 0, A.is_equal, ["t1"], ["i2"], -2048.0, A.mult)
     tt(T.su[:], T.su1[:], T.mb[:], A.mult, ["su1", "mb"], ["su"])
+    tt(T.su2[:], T.su[:], T.i2[:], A.add, ["su", "i2"], ["su2"])
     for n in range(4):
         cpy(T.xa[:, qs[n]], T.xi[:, qs[n]], [("xi", n)], [("x", 0, n // 2)])
-    tt(T.su2[:], T.su[:], T.i2[:], A.add, ["su", "i2"], ["su2"])
-    ts(T.rw[:], T.ri[:], -1.0, A.mult, ["ri"], ["rw"])
     dma("Y", T.dat[1:128:16, :], T.lo[0:8, :], ["lo"], ["dat"])
     dma("Y", T.er[0:8, :], T.mb[0:128:16, :], ["mb"], ["er"])
-    dma("Y", T.rneg[0:8, :], T.rw[:], ["rw"], ["rneg"])
 
-    def total(t):
+    def total(t, h):
         x = xs[t % 2]
         for i in range(16):
-            mmul(T.tc[:, 0:64], T.bp[:, 16 - i:144 - i], x[:, i:P:16], i == 0, i == 15,
-                 ["bp", ("x", t % 2, 0), ("x", t % 2, 1)], ["tc"])
+            mmul(T["tc%d" % h][:, 0:32], T.bp[:, 16 - i:144 - i], x[:, h * H + i:(h + 1) * H:16], i == 0, i == 15,
+                 ["bp", ("x", t % 2, h)], [("tc", h)])
 
-    def flag(t, between):
-        x = xs[t % 2]
-        tc = T.tc
-        ill, illk = ills[t % 2], ("ill", t % 2)
-        ts(T.high[:], tc[:, 0:64], float(TH), A.is_ge, ["tc"], ["high"])
-        for n, l in ((1, "mb"), (2, "su2"), (3, "su")):
-            mmul(tc[:, 64 * n:64 * n + 64], T[l][:], T.high[:], True, True, [l, "high"], ["tc"])
-        for h in (0, 1):
-            mmul(T["e%d" % h][:], T.idn[:], x[:, hs[h]], True, False, ["idn", ("x", t % 2, h)], ["e%d" % h])
-        emit("V", lambda: g.vector.tensor_tensor_scan(T.pre[:], tc[:, 64:128], T.z64[:], 0.0, A.add, A.add),
-             ["tc", "z64"], ["pre"])
-        act(T.cw[:, t:t + 1], T.pre[:, 63:64], F.Relu, ["pre"], [("cw", t)], scale=-1.0, bias=float(CAP))
-        tt(T.zz[:], T.pre[:], tc[:, 128:192], A.add, ["pre", "tc"], ["zz"])
-        ts(ill[:], T.zz[:], CAP - 2048 + 0.5, A.is_le, ["zz"], [illk])
-        between()
-        if right:
-            act(T.sel[:], ill[:], F.Copy, [illk], ["sel"], scale=-float(P), bias=float(P))
+    def high(t, h):
+        ts(T.high[:, cs[h]], T["tc%d" % h][:, 0:32], float(TH), A.is_ge, [("tc", h)], [("high", h)])
+
+    def running(t, h):
+        tc = T["tc%d" % h]
+        for n, l in ((1, "mb"), (2, "su2")):
+            mmul(tc[:, 32 * n:32 * n + 32], T[l][:], T.high[:, cs[h]], True, True, [l, ("high", h)], [("tc", h)])
+        if h == 1:
+            mmul(tc[:, 96:160], T.su[:], T.high[:], True, True, ["su", ("high", 0), ("high", 1)], [("tc", 1)])
+        mmul(T["e%d" % h][:], T.idn[:], xs[t % 2][:, hs[h]], True, False, ["idn", ("x", t % 2, h)], ["e%d" % h])
+
+    def infected(t, h):
+        tc, tk = T["tc%d" % h], ("tc", h)
+        init = 0.0 if h == 0 else T.pre[:, 31:32]
+        emit("V", lambda: g.vector.tensor_tensor_scan(T.pre[:, cs[h]], tc[:, 32:64], T.z64[:, 0:32], init, A.add, A.add),
+             [tk, "z64"] + [("pre", 0)] * h, [("pre", h)])
+        tt(T.zz[:, cs[h]], T.pre[:, cs[h]], tc[:, 64:96], A.add, [("pre", h), tk], [("zz", h)])
+        ts(ills[t % 2][:, cs[h]], T.zz[:, cs[h]], CAP - 2048 + 0.5, A.is_le, [("zz", h)], [("ill", t % 2, h)])
+
+    def spread(t, h):
+        e = T["e%d" % h]
+        for i in range(16):
+            mmul(e[:, i:H:16], T.ex[:, i * 128:(i + 1) * 128], ills[t % 2][:, cs[h]], False, i == 15,
+                 [("ex", i), ("ill", t % 2, h)], ["e%d" % h])
+
+    def mask(t, h):
+        o = T["win%d" % t][:, q * P + h * H:q * P + (h + 1) * H]
+        e = T["e%d" % h]
+        if MQ[h] == "V":
+            ts(o, e[:], -256.0, A.add, ["e%d" % h], [("win", t, h)], 0.0, A.max)
         else:
-            act(T.sel[:], ill[:], F.Copy, [illk], ["sel"], scale=float(P))
-        w = T["win%d" % t]
-        for h in (0, 1):
-            e = T["e%d" % h]
-            for i in range(16):
-                mmul(e[:, i:H:16], T.ex[:, i * 128:(i + 1) * 128], ill[:, 32 * h:32 * h + 32], False, i == 15,
-                     [("ex", i), illk], ["e%d" % h])
-            o = w[:, q * P + h * H:q * P + (h + 1) * H]
-            if h == 0:
-                ts(o, e[:], -256.0, A.add, ["e0"], [("win", t, 0)], 0.0, A.max)
+            act(o, e[:], F.Relu, ["e%d" % h], [("win", t, h)], bias=-256.0)
+        send(o, o, "%s%d" % (("al", "ah")[h], t), [("win", t, h)])
+
+    def counts(t, j):
+        b = 16 * t + 4 * q
+        c = T.cnt[:, b + 1:b + 2]
+        if j == 0:
+            ts(c, T.pre[:, 63:64], float(CAP), A.min, [("pre", 1)], [("cn", t, 1)])
+            return
+        ts(T.cnt[:, b:b + 1], c, -1.0 / 2048, A.mult, [("cn", t, 1)], [("cn", t, 0)], 0.5, A.add)
+        m, a = (1.0, EPS - 0.5) if q == 0 else (-1.0, 2047.5)
+        ts(T.cnt[:, b + 2:b + 3], c, m, A.mult, [("cn", t, 1)], [("cn", t, 2)], a, A.add)
+        s = T.cnt[:, b:b + 3]
+        send(s, s, "ac%d" % t, [("cn", t, 0), ("cn", t, 1), ("cn", t, 2)])
+
+    def spots(t, j):
+        ill = ills[t % 2]
+        ik = [("ill", t % 2, 0), ("ill", t % 2, 1)]
+        if j == 0:
+            tt(T.cum[:], T.pre[:], T.tc1[:, 96:160], A.add, [("pre", 0), ("pre", 1), ("tc", 1)], ["cum"])
+        elif j == 1:
+            if right:
+                ts(T.sel[:], ill[:], -float(P), A.mult, ik, ["sel"], float(P), A.add)
             else:
-                act(o, e[:], F.Relu, ["e1"], [("win", t, 1)], bias=-256.0)
-        seg = w[:, q * P:(q + 1) * P]
-        send(seg, seg, "al%d" % t, [("win", t, 0), ("win", t, 1)])
-        send(T.cnt[:, 4 * t + q:4 * t + q + 1], T.cw[:, t:t + 1], "ac%d" % t, [("cw", t)])
-
-    def scatter(t):
-        tt(T.cum[:], T.pre[:], T.tc[:, 192:256], A.add, ["pre", "tc"], ["cum"])
-        if right:
-            ts(T.cum[:], T.cum[:], float(CAP), A.min, ["cum"], ["cum"], -float(CAP), A.add)
-        else:
-            ts(T.cum[:], T.cum[:], float(CAP), A.min, ["cum"], ["cum"])
-        tt(T.ee[:], T.sel[:], T.vv[:], A.min if right else A.max, ["sel", "vv"], ["ee"])
-        tt(T.pos[:], T.ee[:], T.cum[:], A.subtract, ["ee", "cum"], ["pos"])
-        if right:
-            ts(T.pos16[:], T.pos[:], T.cw[:, t:t + 1], A.subtract, ["pos", ("cw", t)], ["pos16"])
+                ts(T.sel[:], ill[:], float(P), A.mult, ik, ["sel"])
+        elif j == 2:
+            if right:
+                ts(T.cum[:], T.cum[:], float(CAP), A.min, ["cum"], ["cum"], -float(CAP), A.add)
+            else:
+                ts(T.cum[:], T.cum[:], float(CAP), A.min, ["cum"], ["cum"])
+        elif j == 3:
+            tt(T.ee[:], T.sel[:], T.vv[:], A.min if right else A.max, ["sel", "vv"], ["ee"])
+        elif j == 4:
+            tt(T.pos[:], T.ee[:], T.cum[:], A.subtract, ["ee", "cum"], ["pos"])
+        elif right:
+            b = 16 * t + 4 * q
+            ts(T.pos16[:], T.pos[:], T.cnt[:, b + 1:b + 2], A.add, ["pos", ("cn", t, 1)], ["pos16"], -float(CAP), A.add)
         else:
             cpy(T.pos16[:], T.pos[:], ["pos"], ["pos16"])
+
+    def scatter(t):
         seg = T["sw%d" % t][:, q * P:(q + 1) * P]
         emit("V", lambda: g.vector.tensor_copy(seg.indirect(T.pos16[:, 0:64]), T.dat[:]), ["pos16", "dat"], [("sw", t, "own")])
         send(seg, seg, "as%d" % t, [("sw", t, "own")])
 
-    def columns(t):
-        c = [T.cw[:, t:t + 1] if r == q else T.cnt[:, 4 * t + r:4 * t + r + 1] for r in range(4)]
-        rd = [("cw", t), ("cnt", t)]
-        k = T.col
-        f = 1.0 / 2048
-        act(k[:, 0:1], c[0], F.Copy, rd, ["k0"], scale=f, bias=1.25)
-        act(k[:, 4:5], c[1], F.Copy, rd, ["k4"], scale=-1.0, bias=2.0 * CAP)
-        act(k[:, 6:7], c[0], F.Copy, rd, ["k6"], scale=-1.0, bias=CAP - 0.5 + EPS)
-        act(k[:, 1:2], c[1], F.Identity, rd + ["k0"], ["k1"], scale=f, bias=k[:, 0:1])
-        act(k[:, 5:6], c[2], F.Identity, rd + ["k4"], ["k5"], scale=-1.0, bias=k[:, 4:5])
-        act(k[:, 7:8], c[1], F.Copy, rd, ["k7"], bias=2047.5 - CAP)
-        act(k[:, 2:3], c[2], F.Identity, rd + ["k1"], ["k2"], scale=f, bias=k[:, 1:2])
-        act(k[:, 3:4], c[3], F.Identity, rd + ["k2"], ["k3"], scale=f, bias=k[:, 2:3])
+    def places(t, j):
+        b = 16 * t
+        rd = [("cn", t, 0), ("cn", t, 1), ("cn", t, 2), ("cnt", t, "rem")]
+        y = T.sl[:, 256:512]
+        if j == 0:
+            emit("V", lambda: g.vector.tensor_reduce(T.ka[:, t:t + 1], T.cnt[:, b:b + 13:4], X.X, A.add), rd, [("ka", t)])
+            emit("V", lambda: g.vector.tensor_reduce(T.kb[:, t:t + 1], T.cnt[:, b + 5:b + 10:4], X.X, A.add), rd, [("kb", t)])
+        elif j == 1:
+            ts(y, T["dd%d" % t][:], T.ka[:, t:t + 1], A.mult, [("dd", t), ("ka", t)] + rd, ["sl"], T.cnt[:, b + 2:b + 3], A.add)
+        elif j == 2:
+            ts(T.hh[:], y, T.cnt[:, b + 6:b + 7], A.is_ge, ["sl", ("kb", t)] + rd, ["hh"], T.kb[:, t:t + 1], A.mult)
+        elif j == 3:
+            tt(T.oi[:], y, T.hh[:], A.add, ["sl", "hh"], ["oi"])
+        else:
+            cpy(T["offs%d" % (t % 2)][:], T.oi[:], ["oi"], [("offs", t % 2)])
 
-    def places(t):
-        k = T.col
-        y = T.e1[:, 0:256]
-        d, dk = (T.di, "di") if t == 0 else (T["dd%d" % t], ("dd", t))
-        ts(y, d[:], k[:, 3:4], A.mult, [dk, "k3", "k6"], ["e1"], k[:, 6:7], A.add)
-        ts(T.hh[:], y, k[:, 7:8], A.is_ge, ["e1", "k7", "k5"], ["hh"], k[:, 5:6], A.mult)
-        tt(T.oi[:], y, T.hh[:], A.add, ["e1", "hh"], ["oi"])
-        cpy(T["offs%d" % (t % 2)][:], T.oi[:], ["oi"], [("offs", t % 2)])
-
-    def draws(t):
-        ts(T.dtmp[:], T.di[:], STEP * t, A.add, ["di"], ["dtmp"])
-        ts(T["dd%d" % t][:], T.dtmp[:], M2, A.bitwise_and, ["dtmp"], [("dd", t)])
-
-    def sums(bank, key, lhs, src, srck, k, i0, i1, extra):
-        o = bank[:, 64 * k:64 * k + 64]
+    def sums(o, key, lhs, src, srck, h, i0, i1):
         for i in range(i0, i1):
-            mmul(o, lhs[0][:, 16 - i:144 - i], src[:, k * P + i:(k + 1) * P:16], i == 0, False,
-                 [lhs[1], (srck, k, 0), (srck, k, 1)], [key])
+            mmul(o, lhs[0][:, 16 - i:144 - i], src[:, h * 4 * H + i:(h + 1) * 4 * H:16], i == 0, False,
+                 [lhs[1]] + [(srck, k, h) for k in range(4)], [key])
+
+    def hits(t, h, part=None):
+        i0, i1 = (0, 16) if part is None else (8 * part, 8 * part + 8)
+        sums(T.ht[:, ks[h]], "ht", (T.bp, "bp"), T.raw, "raw", h, i0, i1)
         if i1 == 16:
-            l, lk, rhs, rk = extra
-            mmul(o, l[:], rhs, False, True, [lk, rk], [key])
+            for k in range(4):
+                mmul(T.ht[:, own(h, k)], T.ineg[:], ills[t % 2][:, cs[h]], False, k == 3, ["ineg", ("ill", t % 2, h)], ["ht"])
 
-    def hits(t, k, i0=0, i1=16):
-        sums(T.ht, "ht", (T.bp, "bp"), T.raw, "raw", k, i0, i1, (T.ineg, "ineg", ills[t % 2][:], ("ill", t % 2)))
+    SB = [("sl", T.sl), ("c1", T.c1)]
 
-    def slsum(t, k):
+    def slsum(t, h):
         l = ("idn", "id2", "id3", "id4")[t]
-        b = "sl" if k < 2 else "c2"
-        sums(T[b], b, (T.cp, "cp"), T.rsl, "rsl", k, 0, 16, (T[l], l, T.sg[:, 64 * k:64 * k + 64], "sg"))
+        b, B = SB[h]
+        o = B[:, ks[0]]
+        sums(o, b, (T.cp, "cp"), T.rsl, "rsl", h, 0, 16)
+        mmul(o, T[l][:], T.sg[:, ks[h]], False, True, [l, ("sg", h)], [b])
 
     def fetch(qn, win, wk, offs, ok, out, outk, k, h):
-        o = out[:, k * P + h * H:k * P + (h + 1) * H]
-        s = win[:].indirect(offs[:, 64 * k + 32 * h:64 * k + 32 * h + 32])
+        o = out[:, h * 4 * H + k * H:h * 4 * H + (k + 1) * H]
+        s = win[:].indirect(offs[:, own(h, k)])
         if qn == "V":
             cpy(o, s, wk + [ok], [(outk, k, h)])
         else:
             act(o, s, F.Copy, wk + [ok], [(outk, k, h)])
 
-    def loads(t):
-        w = T["win%d" % t]
-        wk = [("win", t, 0), ("win", t, 1), ("win", t, "rem")]
-        nx = (t + 1) % 2
+    def gather(t, k, h):
+        wk = [("win", t, 0), ("win", t, 1), ("win", t, 0, "rem"), ("win", t, 1, "rem")]
+        fetch((LQ if t < DAYS - 1 else LQL)["%d%d" % (k, h)], T["win%d" % t], wk, T.off, ("off", h), T.raw, "raw", k, h)
+
+    def slfetch(t, k, h):
+        wk = [("sw", t, "own"), ("sw", t, "rem")]
+        fetch((SQ if t < DAYS - 1 else SQL)["%d%d" % (k, h)], T["sw%d" % t], wk, T["offs%d" % (t % 2)], ("offs", t % 2),
+              T.rsl, "rsl", k, h)
+
+    banks = ["c0", "c1"]
+    nb = [0]
+
+    def bank():
+        nb[0] += 1
+        return banks[(nb[0] - 1) % 2]
+
+    def raws(k, h):
+        return T.raw[:, h * 4 * H + k * H:h * 4 * H + (k + 1) * H]
+
+    def lift(k, h):
+        b = bank()
+        mmul(T[b][:], T.idn[:], raws(k, h), True, True, ["idn", ("raw", k, h)], [b])
+        a = raws(0, h) if k == 1 else T.mm[:, hs[h]]
+        tt(T.mm[:, hs[h]], a, T[b][:], A.max, [("raw", 0, h) if k == 1 else ("mm", h), b], [("mm", h)])
+
+    def resist(h):
+        mmul(T["e%d" % h][:], T.er[:], T.rneg[:, hs[h]], True, False, ["er", "rneg"], ["e%d" % h])
+
+    def less(h):
+        mmul(T["e%d" % h][:], T.idn[:], T.mm[:, hs[h]], False, True, ["idn", ("mm", h)], ["e%d" % h])
+        tt(T.xm[:, hs[h]], T.xm[:, hs[h]], T["e%d" % h][:], A.max, [("xm", h), "e%d" % h], [("xm", h)])
+
+    def newx(t, h):
         last = t == DAYS - 1
-        for n, (k, h) in enumerate(VG):
-            if n == 1 and t > 0:
-                renew(t - 1, 1)
-            fetch("V", w, wk, T.off, ("off", k // 2), T.raw, "raw", k, h)
-        for k, h in SG:
-            fetch("S", w, wk, T.off, ("off", k // 2), T.raw, "raw", k, h)
-            if (k, h) == (2, 1):
-                columns(t)
-        banks = ["c0", "c1", "c2"]
-        nb = [0]
+        nx = (t + 1) % 2
+        o = T.yo if last else xs[nx]
+        b = bank()
+        mmul(T[b][:], T.er[:], T.rneg[:, hs[h]], True, False, ["er", "rneg"], [b])
+        mmul(T[b][:], T.idn[:], raws(3, h), False, True, ["idn", ("raw", 3, h)], [b])
+        tt(o[:, hs[h]], T.xm[:, hs[h]], T[b][:], A.max, [("xm", h), b], [("yo", h) if last else ("x", nx, h)])
+        if last:
+            dma("Y", T.yx[:, hs[h]], T.yo[:, hs[h]], [("yo", h)], [("yx", h)])
 
-        def lift(k, h):
-            b = banks[nb[0] % 3]
-            nb[0] += 1
-            mmul(T[b][:], T.idn[:], T.raw[:, k * P + h * H:k * P + (h + 1) * H], True, True, ["idn", ("raw", k, h)], [b])
-            a = T.raw[:, hs[h]] if k == 1 else T.mm[:, hs[h]]
-            tt(T.mm[:, hs[h]], a, T[b][:], A.max, [("raw", 0, h) if k == 1 else ("mm", h), b], [("mm", h)])
+    def fade(t, h):
+        ts(T.xm[:, hs[h]], xs[t % 2][:, hs[h]], -8.0, A.add, [("x", t % 2, h)], [("xm", h)], 0.0, A.max)
 
-        def resist(h):
-            mmul(T["e%d" % h][:], T.er[:], T.rneg[:, hs[h]], True, False, ["er", "rneg"], ["e%d" % h])
+    def struck(h):
+        act(T.sg[:, ks[h]], T.ht[:, ks[h]], F.Sign, ["ht"], [("sg", h)], bias=-float(TH) / 2)
 
-        def less(h):
-            mmul(T["e%d" % h][:], T.idn[:], T.mm[:, hs[h]], False, True, ["idn", ("mm", h)], ["e%d" % h])
+    def ll(h):
+        return T.tc1[:, 256 + 128 * h:384 + 128 * h]
 
-        def newx(h):
-            o = T.yo if last else xs[nx]
-            tt(o[:, hs[h]], T.xm[:, hs[h]], T["e%d" % h][:], A.max, ["xm", "e%d" % h], [("yo", h) if last else ("x", nx, h)])
-            if last:
-                dma("Y", T.yx[:, hs[h]], T.yo[:, hs[h]], [("yo", h)], [("yx", h)])
+    def keep(h):
+        tt(T.lk[:, ks[h]], ll(h), T.sg[:, ks[h]], A.subtract, [("tc", 1), ("sg", h)], [("lk", h)])
 
-        lift(1, 0)
-        lift(1, 1)
-        hits(t, 0)
-        lift(2, 0)
-        lift(2, 1)
-        places(t)
-        hits(t, 1)
-        lift(3, 0)
-        resist(0)
-        resist(1)
-        hits(t, 2, 0, 8)
-        lift(3, 1)
-        less(0)
-        hits(t, 2, 8, 16)
-        less(1)
-        newx(0)
-        newx(1)
-        hits(t, 3)
+    def renew(t, h):
+        b, B = SB[h]
+        if t < DAYS - 1:
+            tt(ll(h), T.lk[:, ks[h]], B[:, ks[0]], A.max, [("lk", h), b], [("tc", 1)])
+            return
+        tt(T.lk[:, ks[h]], T.lk[:, ks[h]], B[:, ks[0]], A.max, [("lk", h), b], [("lk", h)])
+        for k in range(4):
+            if k % 2:
+                act(T.no[:, nat(h, k)], T.lk[:, own(h, k)], F.Copy, [("lk", h)], [("no", h, k)], scale=SH, bias=-(t + 1) * SH)
+            else:
+                ts(T.no[:, nat(h, k)], T.lk[:, own(h, k)], -(t + 1.0), A.add, [("lk", h)], [("no", h, k)], SH, A.mult)
 
-    def struck():
-        act(T.sg[:], T.ht[:, 0:256], F.Sign, ["ht"], ["sg"], bias=-float(TH) / 2)
-
-    def keep():
-        tt(T.lk[:], T.ll[:], T.sg[:], A.subtract, [("ll", 0), ("ll", 1), "sg"], ["lk"])
-
-    swk = [[("sw", t, "own"), ("sw", t, "rem")] for t in range(DAYS)]
-
-    def slfetch(qn, t, k, h):
-        fetch(qn, T["sw%d" % t], swk[t], T["offs%d" % (t % 2)], ("offs", t % 2), T.rsl, "rsl", k, h)
-
-    def renew(t, u):
-        b = ("sl", "c2")[u]
-        c = slice(128 * u, 128 * u + 128)
-        tt(T.ll[:, c], T.lk[:, c], T[b][:, c], A.max, ["lk", b], [("ll", u)])
-        if t == DAYS - 1:
-            ts(T.no[:, c], T.ll[:, c], -(t + 1.0), A.add, [("ll", u)], [("no", u)], SH, A.mult)
-        else:
-            ts(T.off[:, c], T.ll[:, c], -(t + 1.0), A.add, [("ll", u)], [("off", u)], SH, A.mult)
-
-    def fade(t):
-        ts(T.xm[:], xs[t % 2][:], -8.0, A.add, [("x", t % 2, 0), ("x", t % 2, 1)], ["xm"], 0.0, A.max)
+    def offnew(t, h):
+        ts(T.off[:, ks[h]], ll(h), -(t + 1.0), A.add, [("tc", 1)], [("off", h)], SH, A.mult)
 
     def number():
         ts(T.pmi[:], T.t1[:, 0:1], 15, A.bitwise_and, ["t1"], ["pmi"])
         cpy(T.pmf[:, 0:1], T.pmi[:], ["pmi"], ["pmf"])
         ts(T.vv[:], T.vvc[:], T.pmf[:, 0:1], A.add, ["vvc", "pmf"], ["vv"])
 
-    total(0)
-    flag(0, number)
-    scatter(0)
-    cpy(T.off[:], T.ni[:], ["ni"], [("off", 0), ("off", 1)])
-    fade(0)
-    act(T.pmf[:, 1:2], T.r16[:, 1:2], F.Copy, ["r16"], ["pmf1"], scale=1.0 / 256 / SH)
-    act(T.ineg[:], T.idn[:], F.Copy, ["idn"], ["ineg"], scale=-SH)
-    act(T.pmf[:, 2:3], T.r16[:, 0:1], F.Identity, ["r16", "pmf1"], ["pmf2"], scale=64.0 / 256 / SH, bias=T.pmf[:, 1:2])
-    for n in (2, 3, 4):
-        act(T["id%d" % n][:], T.idn[:], F.Copy, ["idn"], ["id%d" % n], scale=float(n))
-    act(T.cp[:], T.bp[:], F.Copy, ["bp", "pmf2"], ["cp"], scale=T.pmf[:, 2:3])
-    ts(T.ll[:], T.ni[:], 1.0 / SH, A.mult, ["ni"], [("ll", 0), ("ll", 1)])
-    for t in range(1, DAYS):
-        draws(t)
+    def offsets():
+        for h in (0, 1):
+            for k in range(4):
+                cpy(T.off[:, own(h, k)], T.ni[:, nat(h, k)], ["ni"], [("off", h, k)])
+            lastw[("off", h)] = lastw[("off", h, 3)]
 
+    def draws():
+        for h in (0, 1):
+            for k in range(4):
+                cpy(T.dd0[:, own(h, k)], T.di[:, nat(h, k)], ["di"], [("dd0", h, k)])
+        lastw[("dd", 0)] = lastw[("dd0", 1, 3)]
+        for t in range(1, DAYS):
+            ts(T.dtmp[:], T.dd0[:], STEP * t, A.add, [("dd", 0)], ["dtmp"])
+            ts(T["dd%d" % t][:], T.dtmp[:], M2, A.bitwise_and, ["dtmp"], [("dd", t)])
+
+    def misc():
+        ts(T.rw[:], T.ri[:], -1.0, A.mult, ["ri"], ["rw"])
+        dma("Y", T.rneg[0:8, :], T.rw[:], ["rw"], ["rneg"])
+        act(T.pmf[:, 1:2], T.r16[:, 1:2], F.Copy, ["r16"], ["pmf1"], scale=1.0 / 256 / SH)
+        act(T.ineg[:], T.idn[:], F.Copy, ["idn"], ["ineg"], scale=-SH)
+        act(T.pmf[:, 2:3], T.r16[:, 0:1], F.Identity, ["r16", "pmf1"], ["pmf2"], scale=64.0 / 256 / SH, bias=T.pmf[:, 1:2])
+        for n in (2, 3, 4):
+            act(T["id%d" % n][:], T.idn[:], F.Copy, ["idn"], ["id%d" % n], scale=float(n))
+        act(T.cp[:], T.bp[:], F.Copy, ["bp", "pmf2"], ["cp"], scale=T.pmf[:, 2:3])
+        ts(T.nf[:], T.ni[:], 1.0 / SH, A.mult, ["ni"], ["nf"])
+        for h in (0, 1):
+            for k in range(4):
+                act(T.tc1[:, 256 + 128 * h + 32 * k:288 + 128 * h + 32 * k], T.nf[:, nat(h, k)], F.Copy, ["nf"], [("tc", 1)])
+        draws()
+
+    once = {"num": number, "off": offsets, "misc": misc}
+    flags = {"T": total, "a": high, "F": running, "v": infected, "s": spread, "m": mask, "C": counts, "Z": spots, "M": scatter,
+             "D": fade}
+    halves = {"l": lift, "r": resist, "b": less, "u": struck, "K": keep}
+    both = {"g": gather, "k": slfetch, "n": newx, "S": slsum, "R": renew, "O": offnew, "h": hits, "p": places}
+
+    def run(t, order):
+        for n in order.split():
+            a = [int(c) for c in n[1:] if c.isdigit()]
+            if n in once:
+                once[n]()
+            elif n[0] in flags:
+                flags[n[0]](t + 1, *a)
+            elif n[0] in halves:
+                halves[n[0]](*a)
+            else:
+                both[n[0]](t, *a)
+
+    run(-1, FIRST)
     for t in range(DAYS - 1):
-        loads(t)
-        for n, (k, h) in enumerate(PRE):
-            if n == 2:
-                struck()
-            slfetch("S", t, k, h)
-        total(t + 1)
-        fade(t + 1)
-        flag(t + 1, keep)
-        scatter(t + 1)
-        for k, h in POST:
-            slfetch("S", t, k, h)
-        for k in range(4):
-            slsum(t, k)
-        renew(t, 0)
-
-    t = DAYS - 1
-    loads(t)
-    for k, h in ((0, 0), (0, 1), (1, 0)):
-        slfetch("S", t, k, h)
-    struck()
-    for k, h in ((1, 1), (2, 0)):
-        slfetch("S", t, k, h)
-    for k, h in ((3, 0), (3, 1)):
-        slfetch("V", t, k, h)
-    keep()
-    slfetch("V", t, 2, 1)
-    for k in (0, 1, 3, 2):
-        slsum(t, k)
-    renew(t, 0)
-    renew(t, 1)
-    dma("Y", T.ynb[:], T.no[:], [("no", 0), ("no", 1)], ["ynb"])
+        run(t, DAY)
+    run(DAYS - 1, LAST)
+    dma("Y", T.ynb[:], T.no[:], [("no", h, k) for h in (0, 1) for k in range(4)], ["ynb"])
 
     sync_to("G", [lastw["ynb"], lastw[("yx", 0)], lastw[("yx", 1)]])
     for k in ("V", "S", "P", "G"):

from concourse.bass import DstId, RemoteDMATransfer
from concourse.mybir import AluOpType as A, ActivationFunctionType as F, AxisListType as X

DAYS, P, CAP, TH, STEP, M2 = 4, 1024, 384, 1200, 77, 2047
H = 512
EPS = 2.0 ** -12
SH = 8192.0
LQ = {"00": "V", "10": "S", "20": "S", "30": "S", "01": "S", "11": "S", "21": "S", "31": "S"}
SQ = {"00": "S", "10": "S", "20": "S", "30": "S", "01": "S", "11": "S", "21": "S", "31": "S"}
LQL = {"00": "S", "10": "V", "20": "V", "30": "S", "01": "S", "11": "S", "21": "S", "31": "S"}
SQL = {"00": "S", "10": "S", "20": "S", "30": "V", "01": "S", "11": "V", "21": "V", "31": "S"}
MQ = "VS"
FIRST = """T0 a0 F0 T1 num D1 v0 a1 off s0 m0 F1 v1 misc Z0 Z1 s1 Z2 m1 Z3 C0 Z4 D0 Z5 C1 M"""
DAY = """g00 g10 g20 l10 l20 p0 r0 p1 g11 r1 b0 g30 g01 n0 l11 p2 h00 T0 a0 g21 l21 p3 F0 h01 v0 g31 p4 b1 n1 s0 u0 T1 k31 m0
 k20 a1 D1 F1 k11 D0 v1 k10 s1 k00 Z0 m1 Z1 Z2 k30 C0 k21 Z3 h1 k01 C1 S0 u1 Z4 K0 Z5 M R0 O0 S1 K1 R1 O1"""
LAST = """g10 g30 g00 g20 p0 g11 r0 g01 l10 p1 l20 h00 p2 l11 p3 b0 p4 g31 n0 h01 g21 l21 u0 k10 k30 r1 k00 k11 k20 k01 k31 b1
 h1 u1 k21 n1 K1 S0 K0 S1 R0 R1"""


def _sb(dtype, *names, cols, rows=128):
    return {n: ("sbuf", [rows, cols], dtype) for n in names}


SCRATCH = {}
SCRATCH.update(_sb("int32", "xi", cols=P))
SCRATCH.update(_sb("int32", "ni", "di", "dtmp", "oi", "dd0", "dd1", "dd2", "dd3", cols=256))
SCRATCH.update(_sb("int32", "t1", "t2", "t2s", cols=128))
SCRATCH.update(_sb("int32", "ri", cols=64))
SCRATCH.update(_sb("int32", "t3", cols=16))
SCRATCH.update(_sb("int32", "pmi", cols=1))
SCRATCH.update(_sb("uint16", "off", "offs0", "offs1", cols=256))
SCRATCH.update(_sb("uint16", "pos16", cols=64))
SCRATCH.update(_sb("bfloat16", "xa", "xc", "xm", "mm", "dat", cols=P))
SCRATCH.update(_sb("bfloat16", "raw", "rsl", cols=4 * P))
SCRATCH.update(_sb("bfloat16", *["win%d" % _t for _t in range(DAYS)], *["sw%d" % _t for _t in range(DAYS)], cols=4 * P))
SCRATCH.update(_sb("bfloat16", "rneg", "lo", cols=P, rows=8))
SCRATCH.update(_sb("bfloat16", "er", cols=128, rows=8))
SCRATCH.update(_sb("bfloat16", "ex", cols=2048))
SCRATCH.update(_sb("bfloat16", "sg", cols=256))
SCRATCH.update(_sb("bfloat16", "bp", "cp", cols=144))
SCRATCH.update(_sb("bfloat16", "mb", "idn", "id2", "id3", "id4", "ineg", "su", "su1", "i2", "su2", cols=128))
SCRATCH.update(_sb("bfloat16", "high", "ill0", "ill1", "rw", cols=64))
SCRATCH.update(_sb("float32", "yo", cols=P))
SCRATCH.update(_sb("float32", "no", "lk", "hh", "nf", cols=256))
SCRATCH.update(_sb("float32", "pre", "zz", "cum", "ee", "pos", "z64", "vvc", "vv", "sel", cols=64))
SCRATCH.update(_sb("float32", "cnt", cols=16 * DAYS))
SCRATCH.update(_sb("float32", "r16", cols=16))
SCRATCH.update(_sb("float32", "pmf", "ka", "kb", cols=4))
for _b in ("c0", "c1", "e0", "e1", "ht", "sl", "tc0", "tc1"):
    SCRATCH[_b] = ("psum", [128, 512], "float32")
SEMAPHORES = ["pv", "ps", "pp", "pg", "sent"] + ["dm%d" % i for i in range(16)]
SEMAPHORES += [k + "%d" % t for k in ("al", "ah", "ac", "as") for t in range(DAYS)]


def plan(topo, cores, src):
    far = [d for d in cores if d != src and topo.chip(d) != topo.chip(src)]
    near = [d for d in cores if d != src and topo.chip(d) == topo.chip(src)]
    e = {}
    used = []
    for n, d in enumerate(far):
        es = topo.engines(src, d)
        w = len(es) // len(far)
        e[d] = es[n * w:(n + 1) * w]
        used += e[d]
    for n, d in enumerate(near):
        es = [x for x in topo.engines(src, d) if x not in used]
        w = len(es) // len(near)
        e[d] = es[n * w:(n + 1) * w]
    return e


def rank_program(g, core, T, topo):
    q = T.rank_of(core)
    if q is None:
        return
    cores = list(T.cores)
    right = q % 2 == 0
    eng = {c: plan(topo, cores, c) for c in cores}
    queue = {"V": g.vector, "S": g.scalar, "P": g.tensor, "G": g, "Y": g.sync}
    psem = {"V": "pv", "S": "ps", "P": "pp", "G": "pg"}
    done = {k: 0 for k in queue}
    known = {k: {} for k in queue}
    lastw, readers = {}, {}
    ndma = [0]
    nsent = [0]

    def sync_to(qn, toks):
        need = {}
        for t in toks:
            if known[qn].get(t[0], 0) < t[1]:
                if t[1] > need.get(t[0], (0,))[0]:
                    need[t[0]] = (t[1], t)
        for s in sorted(need):
            v, t = need[s]
            if any(o != s and need[o][1][2].get(s, 0) >= v for o in need):
                continue
            queue[qn].wait_ge(T.sem[s], v)
        for s in need:
            v, t = need[s]
            for k2, v2 in t[2].items():
                if known[qn].get(k2, 0) < v2:
                    known[qn][k2] = v2
            if known[qn].get(s, 0) < v:
                known[qn][s] = v

    def deps(qn, reads, writes, accum):
        toks = [lastw[k] for k in reads if k in lastw]
        for k in writes:
            if k in lastw and not (accum and lastw[k][3] == qn):
                toks.append(lastw[k])
            toks += readers.get(k, [])
        sync_to(qn, toks)

    def record(tok, reads, writes):
        for k in reads:
            readers.setdefault(k, []).append(tok)
        for k in writes:
            lastw[k] = tok
            readers[k] = []

    def emit(qn, fn, reads, writes, accum=False):
        deps(qn, reads, writes, accum)
        s = psem[qn]
        fn().then_inc(T.sem[s], 1)
        done[qn] += 1
        record((s, done[qn], dict(known[qn]), qn), reads, writes)

    def dma(qn, out, in_, reads, writes):
        deps(qn, reads, writes, False)
        s = "dm%d" % ndma[0]
        ndma[0] += 1
        queue[qn].dma_start(out, in_).then_inc(T.sem[s], 16)
        record((s, 16, dict(known[qn]), None), reads, writes)

    def send(dst_ap, src_ap, sem, reads):
        deps("G", reads, [], False)
        tr = []
        for d in cores:
            if d == core:
                continue
            rid, pid, se = topo.addr(d)
            es = eng[core][d]
            tr.append(RemoteDMATransfer(src=src_ap, dst=dst_ap, dst_ids=[DstId(rid=rid, pnc=pid)],
                                        dma_engine_mask=sum(1 << x for x in es), remote_sem=T.sem[sem]))
            nsent[0] += len(es)
        g.remote_dma_fused(tr, local_sem=T.sem.sent)

    arrive = sum(len(eng[c][core]) for c in cores if c != core)
    for t in range(DAYS):
        lastw[("win", t, 0, "rem")] = ("al%d" % t, arrive, {}, None)
        lastw[("win", t, 1, "rem")] = ("ah%d" % t, arrive, {}, None)
        lastw[("cnt", t, "rem")] = ("ac%d" % t, arrive, {}, None)
        lastw[("sw", t, "rem")] = ("as%d" % t, arrive, {}, None)

    def ts(out, in0, s1, op0, r, w, s2=None, op1=None):
        if op1 is None:
            emit("V", lambda: g.vector.tensor_scalar(out, in0, s1, None, op0), r, w)
        else:
            emit("V", lambda: g.vector.tensor_scalar(out, in0, s1, s2, op0, op1), r, w)

    def tt(out, a, b, op, r, w):
        emit("V", lambda: g.vector.tensor_tensor(out, a, b, op), r, w)

    def cpy(out, a, r, w):
        emit("V", lambda: g.vector.tensor_copy(out, a), r, w)

    def mmul(out, l, rhs, start, stop, r, w):
        emit("P", lambda: g.tensor.matmul(out, l, rhs, start, stop), r, w, accum=not start)

    def act(out, a, f, r, w, **kw):
        emit("S", lambda: g.scalar.activation(out, a, f, **kw), r, w)

    xs = [T.xa, T.xc]
    ills = [T.ill0, T.ill1]
    hs = [slice(0, H), slice(H, P)]
    cs = [slice(0, 32), slice(32, 64)]
    ks = [slice(0, 128), slice(128, 256)]
    qs = [slice(n * 256, n * 256 + 256) for n in range(4)]

    def nat(h, k):
        return slice(64 * k + 32 * h, 64 * k + 32 * h + 32)

    def own(h, k):
        return slice(128 * h + 32 * k, 128 * h + 32 * k + 32)

    for n in range(4):
        dma("YS"[n % 2], T.xi[:, qs[n]], T.x0[:, qs[n]], [], [("xi", n)])
    dma("Y", T.ni[:], T.nb[:], [], ["ni"])
    dma("S", T.di[:], T.dice[:], [], ["di"])
    dma("Y", T.ri[:], T.res[:], [], ["ri"])

    emit("G", lambda: g.iota(T.t2[:], [[-16, 8], [0, 16]], 0, 1), [], ["t2"])
    emit("G", lambda: g.iota(T.t1[:], [[-1, 128]], 0, 1), [], ["t1"])
    emit("G", lambda: g.iota(T.vvc[:], [[16, 64]], 0, 0, allow_small_or_imprecise_dtypes=True), [], ["vvc"])
    emit("G", lambda: g.iota(T.lo[:], [[0, 16], [1, 64]], 0, 0, allow_small_or_imprecise_dtypes=True), [], ["lo"])
    emit("G", lambda: g.iota(T.dat[:], [[1, 16], [0, 64]], 16 * q, 0, allow_small_or_imprecise_dtypes=True), [], ["dat"])
    emit("V", lambda: g.vector.memset(T.bp[:], 0.0), [], ["bp"])
    emit("V", lambda: g.vector.memset(T.z64[:], 0.0), [], ["z64"])
    ts(T.t2s[:], T.t2[:], 4, A.arith_shift_right, ["t2"], ["t2s"])
    ts(T.t3[:], T.t1[:, 0:16], 15, A.bitwise_and, ["t1"], ["t3"])
    ts(T.mb[:], T.t2s[:], 0, A.is_equal, ["t2s"], ["mb"])
    ts(T.r16[:], T.t3[:], 0, A.is_equal, ["t3"], ["r16"], 256.0, A.mult)
    cpy(T.bp[:, 16:144:16], T.mb[:, 0:128:16], ["mb"], ["bp"])
    for i in range(16):
        act(T.ex[:, i * 128:(i + 1) * 128], T.mb[:], F.Copy, ["mb", "r16"], [("ex", i)], scale=T.r16[:, i:i + 1])
    ts(T.idn[:], T.t1[:], 0, A.is_equal, ["t1"], ["idn"])
    ts(T.su1[:], T.t1[:], 0, A.is_gt, ["t1"], ["su1"], -1.0, A.mult)
    ts(T.i2[:], T.t1[:], 0, A.is_equal, ["t1"], ["i2"], -2048.0, A.mult)
    tt(T.su[:], T.su1[:], T.mb[:], A.mult, ["su1", "mb"], ["su"])
    tt(T.su2[:], T.su[:], T.i2[:], A.add, ["su", "i2"], ["su2"])
    for n in range(4):
        cpy(T.xa[:, qs[n]], T.xi[:, qs[n]], [("xi", n)], [("x", 0, n // 2)])
    dma("Y", T.dat[1:128:16, :], T.lo[0:8, :], ["lo"], ["dat"])
    dma("Y", T.er[0:8, :], T.mb[0:128:16, :], ["mb"], ["er"])

    def total(t, h):
        x = xs[t % 2]
        for i in range(16):
            mmul(T["tc%d" % h][:, 0:32], T.bp[:, 16 - i:144 - i], x[:, h * H + i:(h + 1) * H:16], i == 0, i == 15,
                 ["bp", ("x", t % 2, h)], [("tc", h)])

    def high(t, h):
        ts(T.high[:, cs[h]], T["tc%d" % h][:, 0:32], float(TH), A.is_ge, [("tc", h)], [("high", h)])

    def running(t, h):
        tc = T["tc%d" % h]
        for n, l in ((1, "mb"), (2, "su2")):
            mmul(tc[:, 32 * n:32 * n + 32], T[l][:], T.high[:, cs[h]], True, True, [l, ("high", h)], [("tc", h)])
        if h == 1:
            mmul(tc[:, 96:160], T.su[:], T.high[:], True, True, ["su", ("high", 0), ("high", 1)], [("tc", 1)])
        mmul(T["e%d" % h][:], T.idn[:], xs[t % 2][:, hs[h]], True, False, ["idn", ("x", t % 2, h)], ["e%d" % h])

    def infected(t, h):
        tc, tk = T["tc%d" % h], ("tc", h)
        init = 0.0 if h == 0 else T.pre[:, 31:32]
        emit("V", lambda: g.vector.tensor_tensor_scan(T.pre[:, cs[h]], tc[:, 32:64], T.z64[:, 0:32], init, A.add, A.add),
             [tk, "z64"] + [("pre", 0)] * h, [("pre", h)])
        tt(T.zz[:, cs[h]], T.pre[:, cs[h]], tc[:, 64:96], A.add, [("pre", h), tk], [("zz", h)])
        ts(ills[t % 2][:, cs[h]], T.zz[:, cs[h]], CAP - 2048 + 0.5, A.is_le, [("zz", h)], [("ill", t % 2, h)])

    def spread(t, h):
        e = T["e%d" % h]
        for i in range(16):
            mmul(e[:, i:H:16], T.ex[:, i * 128:(i + 1) * 128], ills[t % 2][:, cs[h]], False, i == 15,
                 [("ex", i), ("ill", t % 2, h)], ["e%d" % h])

    def mask(t, h):
        o = T["win%d" % t][:, q * P + h * H:q * P + (h + 1) * H]
        e = T["e%d" % h]
        if MQ[h] == "V":
            ts(o, e[:], -256.0, A.add, ["e%d" % h], [("win", t, h)], 0.0, A.max)
        else:
            act(o, e[:], F.Relu, ["e%d" % h], [("win", t, h)], bias=-256.0)
        send(o, o, "%s%d" % (("al", "ah")[h], t), [("win", t, h)])

    def counts(t, j):
        b = 16 * t + 4 * q
        c = T.cnt[:, b + 1:b + 2]
        if j == 0:
            ts(c, T.pre[:, 63:64], float(CAP), A.min, [("pre", 1)], [("cn", t, 1)])
            return
        ts(T.cnt[:, b:b + 1], c, -1.0 / 2048, A.mult, [("cn", t, 1)], [("cn", t, 0)], 0.5, A.add)
        m, a = (1.0, EPS - 0.5) if q == 0 else (-1.0, 2047.5)
        ts(T.cnt[:, b + 2:b + 3], c, m, A.mult, [("cn", t, 1)], [("cn", t, 2)], a, A.add)
        s = T.cnt[:, b:b + 3]
        send(s, s, "ac%d" % t, [("cn", t, 0), ("cn", t, 1), ("cn", t, 2)])

    def spots(t, j):
        ill = ills[t % 2]
        ik = [("ill", t % 2, 0), ("ill", t % 2, 1)]
        if j == 0:
            tt(T.cum[:], T.pre[:], T.tc1[:, 96:160], A.add, [("pre", 0), ("pre", 1), ("tc", 1)], ["cum"])
        elif j == 1:
            if right:
                ts(T.sel[:], ill[:], -float(P), A.mult, ik, ["sel"], float(P), A.add)
            else:
                ts(T.sel[:], ill[:], float(P), A.mult, ik, ["sel"])
        elif j == 2:
            if right:
                ts(T.cum[:], T.cum[:], float(CAP), A.min, ["cum"], ["cum"], -float(CAP), A.add)
            else:
                ts(T.cum[:], T.cum[:], float(CAP), A.min, ["cum"], ["cum"])
        elif j == 3:
            tt(T.ee[:], T.sel[:], T.vv[:], A.min if right else A.max, ["sel", "vv"], ["ee"])
        elif j == 4:
            tt(T.pos[:], T.ee[:], T.cum[:], A.subtract, ["ee", "cum"], ["pos"])
        elif right:
            b = 16 * t + 4 * q
            ts(T.pos16[:], T.pos[:], T.cnt[:, b + 1:b + 2], A.add, ["pos", ("cn", t, 1)], ["pos16"], -float(CAP), A.add)
        else:
            cpy(T.pos16[:], T.pos[:], ["pos"], ["pos16"])

    def scatter(t):
        seg = T["sw%d" % t][:, q * P:(q + 1) * P]
        emit("V", lambda: g.vector.tensor_copy(seg.indirect(T.pos16[:, 0:64]), T.dat[:]), ["pos16", "dat"], [("sw", t, "own")])
        send(seg, seg, "as%d" % t, [("sw", t, "own")])

    def places(t, j):
        b = 16 * t
        rd = [("cn", t, 0), ("cn", t, 1), ("cn", t, 2), ("cnt", t, "rem")]
        y = T.sl[:, 256:512]
        if j == 0:
            emit("V", lambda: g.vector.tensor_reduce(T.ka[:, t:t + 1], T.cnt[:, b:b + 13:4], X.X, A.add), rd, [("ka", t)])
            emit("V", lambda: g.vector.tensor_reduce(T.kb[:, t:t + 1], T.cnt[:, b + 5:b + 10:4], X.X, A.add), rd, [("kb", t)])
        elif j == 1:
            ts(y, T["dd%d" % t][:], T.ka[:, t:t + 1], A.mult, [("dd", t), ("ka", t)] + rd, ["sl"], T.cnt[:, b + 2:b + 3], A.add)
        elif j == 2:
            ts(T.hh[:], y, T.cnt[:, b + 6:b + 7], A.is_ge, ["sl", ("kb", t)] + rd, ["hh"], T.kb[:, t:t + 1], A.mult)
        elif j == 3:
            tt(T.oi[:], y, T.hh[:], A.add, ["sl", "hh"], ["oi"])
        else:
            cpy(T["offs%d" % (t % 2)][:], T.oi[:], ["oi"], [("offs", t % 2)])

    def sums(o, key, lhs, src, srck, h, i0, i1):
        for i in range(i0, i1):
            mmul(o, lhs[0][:, 16 - i:144 - i], src[:, h * 4 * H + i:(h + 1) * 4 * H:16], i == 0, False,
                 [lhs[1]] + [(srck, k, h) for k in range(4)], [key])

    def hits(t, h, part=None):
        i0, i1 = (0, 16) if part is None else (8 * part, 8 * part + 8)
        sums(T.ht[:, ks[h]], "ht", (T.bp, "bp"), T.raw, "raw", h, i0, i1)
        if i1 == 16:
            for k in range(4):
                mmul(T.ht[:, own(h, k)], T.ineg[:], ills[t % 2][:, cs[h]], False, k == 3, ["ineg", ("ill", t % 2, h)], ["ht"])

    SB = [("sl", T.sl), ("c1", T.c1)]

    def slsum(t, h):
        l = ("idn", "id2", "id3", "id4")[t]
        b, B = SB[h]
        o = B[:, ks[0]]
        sums(o, b, (T.cp, "cp"), T.rsl, "rsl", h, 0, 16)
        mmul(o, T[l][:], T.sg[:, ks[h]], False, True, [l, ("sg", h)], [b])

    def fetch(qn, win, wk, offs, ok, out, outk, k, h):
        o = out[:, h * 4 * H + k * H:h * 4 * H + (k + 1) * H]
        s = win[:].indirect(offs[:, own(h, k)])
        if qn == "V":
            cpy(o, s, wk + [ok], [(outk, k, h)])
        else:
            act(o, s, F.Copy, wk + [ok], [(outk, k, h)])

    def gather(t, k, h):
        wk = [("win", t, 0), ("win", t, 1), ("win", t, 0, "rem"), ("win", t, 1, "rem")]
        fetch((LQ if t < DAYS - 1 else LQL)["%d%d" % (k, h)], T["win%d" % t], wk, T.off, ("off", h), T.raw, "raw", k, h)

    def slfetch(t, k, h):
        wk = [("sw", t, "own"), ("sw", t, "rem")]
        fetch((SQ if t < DAYS - 1 else SQL)["%d%d" % (k, h)], T["sw%d" % t], wk, T["offs%d" % (t % 2)], ("offs", t % 2),
              T.rsl, "rsl", k, h)

    banks = ["c0", "c1"]
    nb = [0]

    def bank():
        nb[0] += 1
        return banks[(nb[0] - 1) % 2]

    def raws(k, h):
        return T.raw[:, h * 4 * H + k * H:h * 4 * H + (k + 1) * H]

    def lift(k, h):
        b = bank()
        mmul(T[b][:], T.idn[:], raws(k, h), True, True, ["idn", ("raw", k, h)], [b])
        a = raws(0, h) if k == 1 else T.mm[:, hs[h]]
        tt(T.mm[:, hs[h]], a, T[b][:], A.max, [("raw", 0, h) if k == 1 else ("mm", h), b], [("mm", h)])

    def resist(h):
        mmul(T["e%d" % h][:], T.er[:], T.rneg[:, hs[h]], True, False, ["er", "rneg"], ["e%d" % h])

    def less(h):
        mmul(T["e%d" % h][:], T.idn[:], T.mm[:, hs[h]], False, True, ["idn", ("mm", h)], ["e%d" % h])
        tt(T.xm[:, hs[h]], T.xm[:, hs[h]], T["e%d" % h][:], A.max, [("xm", h), "e%d" % h], [("xm", h)])

    def newx(t, h):
        last = t == DAYS - 1
        nx = (t + 1) % 2
        o = T.yo if last else xs[nx]
        b = bank()
        mmul(T[b][:], T.er[:], T.rneg[:, hs[h]], True, False, ["er", "rneg"], [b])
        mmul(T[b][:], T.idn[:], raws(3, h), False, True, ["idn", ("raw", 3, h)], [b])
        tt(o[:, hs[h]], T.xm[:, hs[h]], T[b][:], A.max, [("xm", h), b], [("yo", h) if last else ("x", nx, h)])
        if last:
            dma("Y", T.yx[:, hs[h]], T.yo[:, hs[h]], [("yo", h)], [("yx", h)])

    def fade(t, h):
        ts(T.xm[:, hs[h]], xs[t % 2][:, hs[h]], -8.0, A.add, [("x", t % 2, h)], [("xm", h)], 0.0, A.max)

    def struck(h):
        act(T.sg[:, ks[h]], T.ht[:, ks[h]], F.Sign, ["ht"], [("sg", h)], bias=-float(TH) / 2)

    def ll(h):
        return T.tc1[:, 256 + 128 * h:384 + 128 * h]

    def keep(h):
        tt(T.lk[:, ks[h]], ll(h), T.sg[:, ks[h]], A.subtract, [("tc", 1), ("sg", h)], [("lk", h)])

    def renew(t, h):
        b, B = SB[h]
        if t < DAYS - 1:
            tt(ll(h), T.lk[:, ks[h]], B[:, ks[0]], A.max, [("lk", h), b], [("tc", 1)])
            return
        tt(T.lk[:, ks[h]], T.lk[:, ks[h]], B[:, ks[0]], A.max, [("lk", h), b], [("lk", h)])
        for k in range(4):
            if k % 2:
                act(T.no[:, nat(h, k)], T.lk[:, own(h, k)], F.Copy, [("lk", h)], [("no", h, k)], scale=SH, bias=-(t + 1) * SH)
            else:
                ts(T.no[:, nat(h, k)], T.lk[:, own(h, k)], -(t + 1.0), A.add, [("lk", h)], [("no", h, k)], SH, A.mult)

    def offnew(t, h):
        ts(T.off[:, ks[h]], ll(h), -(t + 1.0), A.add, [("tc", 1)], [("off", h)], SH, A.mult)

    def number():
        ts(T.pmi[:], T.t1[:, 0:1], 15, A.bitwise_and, ["t1"], ["pmi"])
        cpy(T.pmf[:, 0:1], T.pmi[:], ["pmi"], ["pmf"])
        ts(T.vv[:], T.vvc[:], T.pmf[:, 0:1], A.add, ["vvc", "pmf"], ["vv"])

    def offsets():
        for h in (0, 1):
            for k in range(4):
                cpy(T.off[:, own(h, k)], T.ni[:, nat(h, k)], ["ni"], [("off", h, k)])
            lastw[("off", h)] = lastw[("off", h, 3)]

    def draws():
        for h in (0, 1):
            for k in range(4):
                cpy(T.dd0[:, own(h, k)], T.di[:, nat(h, k)], ["di"], [("dd0", h, k)])
        lastw[("dd", 0)] = lastw[("dd0", 1, 3)]
        for t in range(1, DAYS):
            ts(T.dtmp[:], T.dd0[:], STEP * t, A.add, [("dd", 0)], ["dtmp"])
            ts(T["dd%d" % t][:], T.dtmp[:], M2, A.bitwise_and, ["dtmp"], [("dd", t)])

    def misc():
        ts(T.rw[:], T.ri[:], -1.0, A.mult, ["ri"], ["rw"])
        dma("Y", T.rneg[0:8, :], T.rw[:], ["rw"], ["rneg"])
        act(T.pmf[:, 1:2], T.r16[:, 1:2], F.Copy, ["r16"], ["pmf1"], scale=1.0 / 256 / SH)
        act(T.ineg[:], T.idn[:], F.Copy, ["idn"], ["ineg"], scale=-SH)
        act(T.pmf[:, 2:3], T.r16[:, 0:1], F.Identity, ["r16", "pmf1"], ["pmf2"], scale=64.0 / 256 / SH, bias=T.pmf[:, 1:2])
        for n in (2, 3, 4):
            act(T["id%d" % n][:], T.idn[:], F.Copy, ["idn"], ["id%d" % n], scale=float(n))
        act(T.cp[:], T.bp[:], F.Copy, ["bp", "pmf2"], ["cp"], scale=T.pmf[:, 2:3])
        ts(T.nf[:], T.ni[:], 1.0 / SH, A.mult, ["ni"], ["nf"])
        for h in (0, 1):
            for k in range(4):
                act(T.tc1[:, 256 + 128 * h + 32 * k:288 + 128 * h + 32 * k], T.nf[:, nat(h, k)], F.Copy, ["nf"], [("tc", 1)])
        draws()

    once = {"num": number, "off": offsets, "misc": misc}
    flags = {"T": total, "a": high, "F": running, "v": infected, "s": spread, "m": mask, "C": counts, "Z": spots, "M": scatter,
             "D": fade}
    halves = {"l": lift, "r": resist, "b": less, "u": struck, "K": keep}
    both = {"g": gather, "k": slfetch, "n": newx, "S": slsum, "R": renew, "O": offnew, "h": hits, "p": places}

    def run(t, order):
        for n in order.split():
            a = [int(c) for c in n[1:] if c.isdigit()]
            if n in once:
                once[n]()
            elif n[0] in flags:
                flags[n[0]](t + 1, *a)
            elif n[0] in halves:
                halves[n[0]](*a)
            else:
                both[n[0]](t, *a)

    run(-1, FIRST)
    for t in range(DAYS - 1):
        run(t, DAY)
    run(DAYS - 1, LAST)
    dma("Y", T.ynb[:], T.no[:], [("no", h, k) for h in (0, 1) for k in range(4)], ["ynb"])

    sync_to("G", [lastw["ynb"], lastw[("yx", 0)], lastw[("yx", 1)]])
    for k in ("V", "S", "P", "G"):
        g.wait_ge(T.sem[psem[k]], done[k])
    g.wait_ge(T.sem.sent, nsent[0])
